import numpy as np, ml_dtypes
CORES = [25,29,65,69,153,157,193,197]
N = 8
BF = ml_dtypes.bfloat16
def gentries(a):
    return np.ascontiguousarray(a.reshape(8, 16, -1).transpose(0, 2, 1)).reshape(8, -1)
def gtable(e):
    e = np.asarray(e); return np.ascontiguousarray(e.reshape(8, -1, 16).transpose(0, 2, 1)).reshape(128, -1).astype(np.int32)
W, P, RO = 1536, 128, 3
def parts(rng):
    X = rng.integers(0, 128, (N, 8, 16, W)); G = rng.integers(-127, 128, (N, 8, 16, W)); E = rng.integers(0, 2 ** 20, (N, 8, W)); B = rng.integers(0, W, (N, 8, 16, W))
    return X, G, E, B, rng.integers(0, W, (N, 8, P, 16)), rng.integers(0, W, (N, 8, P, 16)), rng.integers(0, 9, (N, 8, P, 16))
def pack(X, G, E, B, a, b, l):
    return {"xrec": np.ascontiguousarray(X.reshape(N, 128, W)).astype(np.float32).astype(BF), "grec": np.ascontiguousarray(G.reshape(N, 128, W)).astype(np.float32).astype(BF),
            "erec": np.ascontiguousarray(E.reshape(N, 8, W)).astype(np.int32), "nbr": np.ascontiguousarray(B.reshape(N, 128, W)).astype(np.int32),
            "pa": np.stack([gtable(t.reshape(8, -1)) for t in a]), "pb": np.stack([gtable(t.reshape(8, -1)) for t in b]), "lam": np.stack([gtable(t.reshape(8, -1)) for t in l])}
def setup_inputs(rng):
    X, G, E, B, a, b, l = parts(rng)
    X[:, 1::2] = (X[:, 1::2] * rng.choice(np.array([1, 4, 16, 16]), (N, 4, 1, W))) >> 4
    E[:, 2::3] &= 2 ** 20 - 2 ** 18
    r = rng.integers(0, W, (N, 8, 1)); a[:, :, 5] = r; b[:, :, 5] = r
    return pack(X, G, E, B, a, b, l)
def setup_inputs_corners(rng):
    X, G, E, B, a, b, l = parts(rng); h = P // 2; sh = int(rng.integers(0, 8)); J = np.arange(16)
    for q in range(N):
        for g in range(8):
            c = (g + q + sh) % 8
            if c == 0:
                z = h // 2; r = rng.integers(0, W, (z, 1)); a[q, g, :z] = r; b[q, g, :z] = r
                rec = rng.permutation(W)[:16]; X[q, g][:, rec] = X[q, g][:, rec[:1]]
                a[q, g, z:h] = rec[rng.integers(0, 16, (h - z, 16))]; b[q, g, z:h] = rec[rng.integers(0, 16, (h - z, 16))]
            elif c == 1:
                B[q, g] = np.arange(W); l[q, g] = 8 * rng.integers(0, 2, (P, 16))
            elif c == 2:
                B[q, g] = (W - 1) * rng.integers(0, 2, (16, W)); l[q, g] = 8 * rng.integers(0, 2, (P, 16))
                a[q, g, :, ::3] = (W - 1) * rng.integers(0, 2, (P, 6)); b[q, g, :, 1::3] = (W - 1) * rng.integers(0, 2, (P, 5))
            elif c == 3:
                l[q, g] = rng.integers(3, 6, (P, 16))
                rec = rng.permutation(W)[:48].reshape(3, 16); o = rng.permutation(16)
                v = 2 * rng.integers(51, 62, (16, 16)); v[o[1]] = v[o[0]]; v[o[2]] = v[o[0]] + 4 * rng.integers(0, 2, 16) - 2
                s = v.copy(); s[o[0]] += 1; s[o[1]] -= 1; u = v >> 1; u[o[0]] += 1; u[o[2]] -= 1
                X[q, g][:, rec[0]] = 0; X[q, g][:, rec[1]] = v; X[q, g][:, rec[2]] = s; G[q, g][:, rec[0]] = u; E[q, g, rec[2]] = 2 ** 20 - 1
                i = np.arange(h) % 16; a[q, g, :h, 0] = rec[0][i]; b[q, g, :h, 0] = rec[1][i]; l[q, g, :h, 0] = 0
                a[q, g, :h, 1] = rec[2][i]; b[q, g, :h, 1] = rec[2][i]
            elif c == 4:
                if q % 2 == 0: E[q, g] = rng.integers(0, 2 ** 20)
                else: E[q, g] = 4096 * int(rng.integers(128, 256)) + 1025 + 8 * int(rng.integers(0, 127)) + rng.integers(0, 2, W)
            elif c == 5:
                G[q, g] = 0; r = rng.integers(0, W, (h, 2))[:, J % 2]; a[q, g, :h] = r; b[q, g, :h] = r
                rec = rng.permutation(W)[:128].reshape(8, 16); inc = np.zeros((16, 16), np.int64); inc[:, 1] = 1; size = rng.permutation(20)[:8] + 1
                for i in range(2, 16): inc[i, i] = 3 if i == 15 else 2
                for i in range(8): X[q, g][:, rec[i]] = 40 + int(size[i]) * np.add.accumulate(inc, axis=1)
                k = rec[np.arange(P - h) % 8]; a[q, g, h:] = k; b[q, g, h:] = k
            elif c == 6:
                r = rng.integers(0, W, (P, 2)); a[q, g] = np.take_along_axis(r, rng.integers(0, 2, (P, 16)), 1); b[q, g] = np.take_along_axis(r, rng.integers(0, 2, (P, 16)), 1)
            else:
                u = rng.integers(0, W, (P, 2)); cut = rng.integers(0, 15, (P, 1)); r = np.where(J <= cut, u[:, :1], u[:, 1:]); a[q, g] = r; k = b[q, g].copy(); b[q, g] = r
                b[q, g, h:, 0] = k[h:, 0]; b[q, g, h:, 15] = k[h:, 15]; l[q, g, h:, 0] = 0; l[q, g, h:, 15] = 0
    return pack(X, G, E, B, a, b, l)
def setup_inputs_crowd(rng):
    X, G, E, B, a, b, l = parts(rng); sh = int(rng.integers(0, 8)); J = np.arange(16)
    for q in range(N):
        for g in range(8):
            c = (g + sh) % 8; one = int(rng.choice(np.array([0, W - 1, int(rng.integers(0, W))])))
            if c < 2:
                B[q, g] = one; l[q, g] = 8 * rng.integers(0, 2, (P, 16))
                if c == 1: B[q, g, int(rng.integers(0, 16)), a[q, g, P - 1, 15]] = (one + 1) % W
            elif c in (2, 3, 6):
                cut = 14 if c == 2 else 13 if c == 3 else 0
                u = rng.integers(0, W, (P, 2)); r = np.where(J <= cut, u[:, :1], u[:, 1:]); k = b[q, g].copy(); a[q, g] = r; b[q, g] = r
                b[q, g, 1::2, 0] = k[1::2, 0]; b[q, g, 1::2, 15] = k[1::2, 15]; l[q, g, 1::2, 0] = 0; l[q, g, 1::2, 15] = 0
            elif c == 4:
                a[q, g] = one; b[q, g] = one; i = int(rng.integers(0, 16)); a[q, g, P - 1, i] = (one + 1) % W; b[q, g, P - 1, i] = (one + 2) % W
            elif c == 5:
                r = rng.integers(0, W, 4); a[q, g] = r[rng.integers(0, 4, (P, 16))]; b[q, g] = r[rng.integers(0, 4, (P, 16))]; B[q, g] = r[rng.integers(0, 4, (16, W))]
            else:
                b[q, g] = one; l[q, g] = 8
    return pack(X, G, E, B, a, b, l)
def setup_inputs_ends(rng):
    X, G, E, B, a, b, l = parts(rng)
    X = 127 * rng.integers(0, 2, X.shape); G = 254 * rng.integers(0, 2, G.shape) - 127; E = (2 ** 20 - 1) * rng.integers(0, 2, E.shape)
    E[:, :, 0] = (2 ** 20 - 1) * rng.integers(0, 2, (N, 8)); E[:, ::2, W - 1] = 2 ** 20 - 1 - E[:, ::2, 0]
    B = np.where(rng.random(B.shape) < 0.3, B, (W - 1) * rng.integers(0, 2, B.shape))
    a = np.where(rng.random(a.shape) < 0.33, a, (W - 1) * rng.integers(0, 2, a.shape)); b = np.where(rng.random(b.shape) < 0.33, b, (W - 1) * rng.integers(0, 2, b.shape))
    l = np.where(rng.random(l.shape) < 0.2, l, 8 * rng.integers(0, 2, l.shape)); alt = (W - 1) * (np.arange(16) % 2)
    for g in (0, 2, 5, 7):
        o = rng.integers(0, 2, (N, 1)); X[:, g, :, 0] = 127 * o; X[:, g, :, W - 1] = 127 * (1 - o)
        s = 254 * rng.integers(0, 2, (N, 2)) - 127
        if g == 7: s[:] = 127
        if g == 0: s[:] = -127
        G[:, g, :, 0] = s[:, :1]; G[:, g, :, W - 1] = s[:, 1:]
        a[:, g, 7::8] = alt; b[:, g, 7::8] = alt
    return pack(X, G, E, B, a, b, l)
def setup_inputs_spread(rng):
    X, G, E, B, a, b, l = parts(rng)
    X = (np.exp2(7 * rng.random((N, 8, 1, W))) * rng.random(X.shape)).astype(np.int64); X[:, 1::2] = 127 - X[:, 1::2]
    G = np.minimum((np.exp2(7 * rng.random((N, 8, 1, W))) * rng.random(G.shape)).astype(np.int64), 127) * (2 * rng.integers(0, 2, G.shape) - 1)
    E = np.minimum(np.exp2(20 * rng.random(E.shape)).astype(np.int64) - 1, 2 ** 20 - 1)
    a = np.minimum((W * rng.random(a.shape) ** 3).astype(np.int64), W - 1); b = np.minimum((W * rng.random(b.shape) ** 2).astype(np.int64), W - 1)
    B = W - 1 - np.minimum((W * rng.random(B.shape) ** 3).astype(np.int64), W - 1)
    l = rng.choice(np.array([0, 0, 0, 1, 2, 3, 4, 4, 5, 6, 7, 8, 8, 8]), l.shape)
    return pack(np.minimum(np.maximum(X, 0), 127), G, E, B, a, b, l)
def check_inputs(d):
    bad = []
    for k, lo, hi in (("xrec", 0, 127), ("grec", -127, 127), ("erec", 0, 2 ** 20 - 1), ("nbr", 0, W - 1), ("pa", 0, W - 1), ("pb", 0, W - 1), ("lam", 0, 8)):
        v = np.asarray(d[k]).astype(np.float64)
        if not (np.min(v) >= lo and np.max(v) <= hi): bad.append("range of " + k)
        elif not np.all(v == np.rint(v)): bad.append("whole numbers in " + k)
    return bad
def pick(t, i):
    return np.take_along_axis(t, i.reshape(N, 8, 1, P * 16), 3).reshape(N, 8, 16, P, 16)
def dot(u, v):
    return np.add.reduce(u * v, axis=2)
def reference(xrec, grec, erec, nbr, pa, pb, lam):
    X = xrec.astype(np.float32).astype(np.int64).reshape(N, 8, 16, W); G = grec.astype(np.float32).astype(np.int64).reshape(N, 8, 16, W)
    E = erec.astype(np.int64); B = nbr.astype(np.int64).reshape(N, 8, 16, W); J = np.arange(16); mid = (J > 0) & (J < 15)
    a, b, l = [np.stack([gentries(t) for t in v]).astype(np.int64).reshape(N, 8, P, 16) for v in (pa, pb, lam)]
    for rnd in range(RO):
        w = l[:, :, None]; xa = pick(X, a); d = pick(X, b) - xa; R = 8 * xa + w * d
        g = (8 - w) * pick(G, a) + w * pick(G, b)
        ea = np.take_along_axis(E, a.reshape(N, 8, P * 16), 2).reshape(N, 8, P, 16); eb = np.take_along_axis(E, b.reshape(N, 8, P * 16), 2).reshape(N, 8, P, 16)
        e = (8 - l) * ea + l * eb
        Rx = np.concatenate([np.roll(R[..., 15:], 1, axis=0), R, np.roll(R[..., :1], -1, axis=0)], axis=4)
        ex = np.concatenate([np.roll(e[..., 15:], 1, axis=0), e, np.roll(e[..., :1], -1, axis=0)], axis=3)
        D = Rx[..., 1:] - Rx[..., :-1]; fwd = ex[..., 2:] >= ex[..., :-2]
        tau = np.where(fwd[:, :, None], D[..., 1:], D[..., :-1])
        p = dot(g, d).astype(np.float32) * dot(tau, tau).astype(np.float32)
        q = dot(g, tau).astype(np.float32) * dot(tau, d).astype(np.float32)
        l = l - (p > q).astype(np.int64) + (p < q).astype(np.int64)
        up = l > 8; dn = l < 0; z = np.where(up, b, a)
        n = np.take_along_axis(B, z.transpose(0, 1, 3, 2), 3).transpose(0, 1, 3, 2)
        a, b, l = np.where(up, b, np.where(dn, n, a)), np.where(up, n, np.where(dn, a, b)), np.where(up, 1, np.where(dn, 7, l))
        xa = pick(X, a); R = 8 * xa + l[:, :, None] * (pick(X, b) - xa)
        H = np.add.reduce(np.abs(R[..., 1:] - R[..., :-1]), axis=2)
        C = np.concatenate([np.zeros((N, 8, P, 1), np.int64), np.add.accumulate(H, axis=3)], axis=3); S = C[..., 15:]
        c = np.where(l <= 4, a, b)
        j = np.add.reduce((15 * C[..., None, :15] <= J[:, None] * S[..., None]).astype(np.int64), axis=4) - 1
        lo = np.take_along_axis(C, j, 3); gap = 15 * (np.take_along_axis(C, j + 1, 3) - lo); rest = 16 * (J * S - 15 * lo); m = np.zeros((N, 8, P, 16), np.int64)
        for i in range(1, 9): m = m + ((2 * i - 1) * gap <= rest)
        a, b, l = np.where(mid, np.take_along_axis(c, j, 3), a), np.where(mid, np.take_along_axis(c, j + 1, 3), b), np.where(mid, m, l)
    ya, yb, yl = [np.stack([gtable(t.reshape(8, -1)) for t in v]).astype(np.float32) for v in (a, b, l)]
    return {"ya": ya, "yb": yb, "yl": yl}

@@ -1,0 +1,773 @@
+import numpy as np
+from concourse.bass import DstId, RemoteDMATransfer
+from concourse.mybir import dt, AluOpType, AxisListType, ActivationFunctionType
+A = AluOpType
+F = ActivationFunctionType
+
+W, RO, NCH = 1536, 3, 2
+H16, B16, F32, I32, U16 = "float16", "bfloat16", "float32", "int32", "uint16"
+MAGIC = 1.5 * 2.0 ** 23
+OPT = {"dg_act": False, "gam": 1.56, "pe": 0.42, "lat": 4500.0, "bias": 4000.0, "act_small": True,
+       "ttg": 0.0, "early": True, "d_act": 0, "t_act": False, "racc": False, "ls_first": False, "th": 0.0, "fbi": 1, "mix": 0.0,
+       "steps": [95816, 31019, 44295, 43595, 72084, 21418, 60966, 94642, 27383, 91537, 87538, 40321, 67301, 11044, 59118, 24142,
+                 23150, 40506, 69720, 71307, 72656, 68659, 90942, 89358, 9372, 9289, 28749, 60054, 26098, 60321, 92555,
+                 30369, 38492, 73172, 85073, 23366, 54715, 49595, 18069, 1629, 72566]}
+REF = {"gam": 1.56, "pe": 0.42, "lat": 4500.0, "ttg": 0.0}
+
+SCRATCH = {
+    "X": ("sbuf", [128, W], B16), "G": ("sbuf", [128, W], B16), "EN": ("sbuf", [128, 2 * W], I32),
+    "e96": ("sbuf", [128, 96], I32), "ehl": ("sbuf", [128, 192], I32), "lin": ("sbuf", [128, 384], I32),
+    "BO": ("sbuf", [128, 128], F32), "IF": ("sbuf", [128, 128], F32), "SH": ("sbuf", [128, 512], F32),
+    "LT": ("sbuf", [128, 128], F32), "BOh": ("sbuf", [128, 128], H16),
+    "ID": ("sbuf", [128, 896], H16), "BC": ("sbuf", [128, 2048], H16), "DG": ("sbuf", [128, 2048], H16),
+    "MD": ("sbuf", [128, 640], H16), "UH": ("sbuf", [128, 144], H16), "UE": ("sbuf", [128, 144], H16),
+    "BO8": ("sbuf", [128, 8], F32), "PMI": ("sbuf", [128, 64], F32), "ONE": ("sbuf", [128, 64], H16),
+    "pi": ("sbuf", [128, 8], I32), "col": ("sbuf", [128, 16], F32), "MK": ("sbuf", [128, 32], F32),
+    "q4": ("sbuf", [128, 512], F32), "WZ": ("sbuf", [128, 896], H16),
+    "WC": ("sbuf", [128, 128], B16), "WH": ("sbuf", [128, 192], B16), "WL": ("sbuf", [128, 256], B16),
+    "NB": ("sbuf", [128, 256], F32), "VE": ("sbuf", [128, 144], H16), "NBh": ("sbuf", [128, 64], H16),
+}
+for _c in range(NCH):
+    for _n, _w, _t in (("abl", 192, H16), ("oab", 128, U16), ("oen", 128, U16), ("ot", 64, U16), ("ou", 64, U16),
+                       ("xa", 1040, B16), ("d", 1024, B16), ("ld", 1024, H16), ("ga", 1024, B16), ("gb", 1024, B16),
+                       ("Ls", 1024, B16), ("lg", 1024, H16), ("en", 2048, H16), ("t", 1024, H16),
+                       ("PA", 2048, F32), ("PB", 2048, F32), ("xu", 1040, B16), ("lp", 1040, H16), ("ad", 1024, H16),
+                       ("sh", 1280, H16), ("sf", 1280, F32), ("si", 448, I32), ("bd", 512, H16), ("pay", 256, F32),
+                       ("nw", 192, H16), ("res", 192, F32), ("eb", 256, H16), ("oe", 16, U16), ("ee", 256, H16)):
+        SCRATCH["%s%d" % (_n, _c)] = ("sbuf", [128, _w], _t)
+    SCRATCH["so%d" % _c] = ("sbuf", [128, 192, 16], F32)
+    for _r in range(RO):
+        SCRATCH["R%d%d" % (_c, _r)] = ("sbuf", [128, 1280], F32)
+        SCRATCH["S%d%d" % (_c, _r)] = ("sbuf", [128, 192], F32)
+for _b in range(8):
+    SCRATCH["bank%d" % _b] = ("psum", [128, 512], F32)
+
+DMAS = ["lx", "lg", "ln", "le", "la", "lb", "ll", "eh", "el"] + ["o%d%d" % (c, q) for c in range(NCH) for q in range(3)]
+SEMAPHORES = ["V", "S", "P", "Q", "sent"] + DMAS + ["h%d%d" % (c, r) for c in range(NCH) for r in range(RO)]
+
+
+def ap(name, c0, c1, st=1, p0=0, p1=128):
+    m = 0
+    if st == 1:
+        m = ((1 << (c1 - c0)) - 1) << c0
+    else:
+        for c in range(c0, c1, st):
+            m |= 1 << c
+    return {"n": name, "i": (slice(p0, p1), slice(c0, c1, st)), "p": (p0, p1), "m": m, "w": len(range(c0, c1, st))}
+
+
+def ap3(name, r0, r1, rs, k0, k1):
+    m = 0
+    for r in range(r0, r1, rs):
+        m |= ((1 << (k1 - k0)) - 1) << (16 * r + k0)
+    idx = (slice(0, 128), slice(r0, r1, rs), k0 if k1 - k0 == 1 else slice(k0, k1))
+    return {"n": name, "i": idx, "p": (0, 128), "m": m, "w": len(range(r0, r1, rs)) * (k1 - k0)}
+
+
+def ind(win, off):
+    return {"win": win, "off": off, "w": 16 * off["w"]}
+
+
+def two(a):
+    return a["n"][:3] != "ps:" and SCRATCH[a["n"]][2] in (H16, B16, U16)
+
+
+def build(opt):
+    ops = []
+    cy = 0.83
+
+    def add(eng, ins, cost, **kw):
+        rd, wr = [], []
+        for kind, args in ins:
+            aps = [x for x in args if isinstance(x, dict)]
+            wr.append(aps[0])
+            for x in aps[1:]:
+                rd.extend([x["win"], x["off"]] if "win" in x else [x])
+        op = {"e": eng, "ins": ins, "c": cost, "rd": rd, "wr": wr, "id": len(ops), "ch": kw.get("ch", -1)}
+        op.update(kw)
+        ops.append(op)
+        return op
+
+    cur = [-1]
+
+    def vcost(out, x, n2):
+        if "win" in x:
+            return 50 + x["w"] * max(opt["gam"], opt["ttg"]) * cy
+        return max(64, x["w"] * n2) * cy
+
+    def tt(out, x, y, o):
+        ps = "win" not in x and (x["n"][:3] == "ps:" or y["n"][:3] == "ps:")
+        add("V", [("tt", (out, x, y, o))], vcost(out, x, 1 if ps else 2), ch=cur[0])
+
+    def ts(out, x, s1, o1, s2=None, o2=None):
+        add("V", [("ts", (out, x, s1, s2, o1, o2))], vcost(out, x, 0.5 if two(out) and two(x) else 1), ch=cur[0])
+
+    def cp(out, x):
+        add("V", [("cp", (out, x))], vcost(out, x, 0.5 if two(out) and two(x) else 1), ch=cur[0])
+
+    def ms(out, v):
+        add("V", [("ms", (out, v))], vcost(out, out, 0.5 if two(out) else 1), ch=cur[0])
+
+    def act(out, x, f=F.Copy, scale=1.0, bias=0.0):
+        c = 65 + x["w"] * opt["gam"] * cy if "win" in x else max(64, x["w"]) * cy
+        add("S", [("act", (out, x, f, bias, scale))], c, ch=cur[0])
+
+    def lin(out, x, scale, bias):
+        if opt["act_small"]:
+            act(out, x, F.Identity if bias else F.Copy, scale, bias)
+        else:
+            ts(out, x, scale, A.mult, bias, A.add)
+
+    def mm(lst):
+        c = 0
+        for out, l, r, s, e in lst:
+            c += max(min(64, l["w"]), r["w"]) * (1 if two(r) else 4) * opt["pe"]
+        add("P", [("mm", x) for x in lst], c, ch=cur[0])
+
+    def grp(out, terms):
+        return [(out, l, r, i == 0, i == len(terms) - 1) for i, (l, r) in enumerate(terms)]
+
+    def sel(out, x, pat, o, base, cm):
+        add("Q", [("sel", (out, x, pat, o, 0.0, base, cm))], 170 + 2 * cy * out["w"])
+
+    def iota(out, pat, base, cm):
+        add("Q", [("iota", (out, pat, base, cm))], 130 + 2 * cy * out["w"])
+
+    def dma(q, sem, out, src, lat):
+        o = {"n": "hbm", "p": (0, 0), "m": 0, "w": 0}
+        add(q, [("dma", (out if isinstance(out, dict) else o, src if isinstance(src, dict) else o, (out, src)))], 60,
+            sem=sem, lat=lat, ch=cur[0])
+
+    dma("Y", "la", ap("lin", 0, 128), ("pa",), 2200)
+    dma("Y", "lx", ap("X", 0, W), ("xrec",), 3200)
+    dma("Y", "lb", ap("lin", 128, 256), ("pb",), 2300)
+    dma("Y", "ll", ap("lin", 256, 384), ("lam",), 2400)
+    dma("Y", "le", ap("e96", 0, 96), ("erec",), 2500)
+    dma("Y", "ln", ap("EN", W, 2 * W), ("nbr",), 5500)
+    dma("Y", "lg", ap("G", 0, W), ("grec",), 6000)
+    ms(ap("EN", 0, W), 0)
+    ts(ap("ehl", 0, 96), ap("e96", 0, 96), 10, A.logical_shift_right)
+    ts(ap("ehl", 96, 192), ap("e96", 0, 96), 1023, A.bitwise_and)
+    for q, sem in ((0, "eh"), (1, "el")):
+        o = ap("EN", 0, W)
+        o["i"] = (slice(q, 128, 16), slice(0, W))
+        o["nowaw"] = True
+        dma("Y", sem, o, ap("ehl", 96 * q, 96 * q + 96), 2200)
+
+    BO, IF = ap("BO", 0, 128), ap("IF", 0, 128)
+    ms(BO, 1.0)
+    ms(IF, 1.0)
+    iota(ap("pi", 0, 1), [[0, 1]], 0, 1)
+    iota(ap("MK", 16, 32), [[1, 16]], 0, 0)
+    sel(IF, IF, [[-1, 128]], A.is_equal, 0, 1)
+    sel(BO, BO, [[-16, 8], [0, 16]], A.is_ge, 0, 1)
+    sel(BO, BO, [[16, 8], [0, 16]], A.is_ge, 15, -1)
+    ts(ap("pi", 4, 5), ap("pi", 0, 1), 15, A.bitwise_and)
+    cp(ap("col", 0, 1), ap("pi", 4, 5))
+    ts(ap("MK", 0, 16), ap("MK", 16, 32), ap("col", 0, 1), A.is_equal)
+    for i, v in enumerate((1.0, 8.0, -1.0, 7.0, -7.0)):
+        ts(ap("ID", 128 * i, 128 * i + 128), IF, v, A.mult)
+    I1, I8, IN, I7, IN7 = [ap("ID", 128 * i, 128 * i + 128) for i in range(5)]
+    cp(ap("BOh", 0, 128), BO)
+    for k in range(16):
+        ts(ap("BC", 128 * k, 128 * k + 128), ap("BOh", 0, 128), ap("MK", k, k + 1), A.mult)
+        act(ap("DG", 128 * k, 128 * k + 128), IF, F.Copy, ap("MK", k, k + 1))
+    ts(ap("col", 1, 2), ap("MK", 0, 1), 1024.0, A.mult, ap("MK", 1, 2), A.add)
+    ts(ap("col", 2, 3), ap("MK", 15, 16), -1.0, A.mult, 1.0, A.add)
+    ts(ap("col", 3, 4), ap("MK", 0, 1), ap("MK", 15, 16), A.add)
+    ms(ap("UH", 0, 144), 0.0)
+    ms(ap("UE", 0, 144), 0.0)
+    ms(ap("ONE", 0, 64), 1.0)
+    ts(ap("UH", 15, 128, 16), ap("BO", 0, 128, 16), 1.0 / 128, A.mult)
+    ts(ap("UE", 15, 128, 16), ap("BO", 0, 128, 16), ap("col", 1, 2), A.mult)
+    ms(ap("VE", 0, 144), 0.0)
+    ts(ap("VE", 15, 128, 16), ap("BO", 0, 128, 16), ap("MK", 0, 1), A.mult)
+    ts(ap("VE", 17, 130, 16), ap("BO", 0, 128, 16), ap("MK", 15, 16), A.mult)
+    cp(ap("BO8", 0, 8), ap("BO", 0, 128, 16))
+    tt(ap("PMI", 0, 64), ap("IF", 64, 128), ap("IF", 0, 64), A.subtract)
+    for i, v in enumerate((1.0, -1.0, 8.0, -7.0)):
+        ts(ap("MD", 128 * i, 128 * i + 128), IF, ap("col", 3, 4), A.mult, v, A.mult)
+    ts(ap("MD", 512, 640), IF, -0.5, A.mult)
+    ts(ap("ID", 640, 768), IF, 1536.0, A.mult)
+    ts(ap("ID", 768, 896), IF, -8.0, A.mult)
+    sel(ap("SH", 384, 512), BO, [[-1, 128]], A.is_equal, -1, 1)
+    sel(ap("SH", 0, 128), BO, [[-1, 128]], A.is_equal, 1, 1)
+    sel(ap("SH", 128, 256), BO, [[-1, 128]], A.is_equal, -15, 1)
+    sel(ap("SH", 256, 384), BO, [[-1, 128]], A.is_equal, 15, 1)
+    sel(ap("LT", 0, 128), BO, [[1, 128]], A.is_gt, 0, -1)
+    tt(ap("SH", 0, 128), ap("SH", 384, 512), ap("SH", 0, 128), A.subtract)
+    ts(ap("SH", 128, 256), ap("SH", 128, 256), -1.0, A.mult)
+    iota(ap("NB", 128, 192), [[16, 64]], 63, 0)
+    iota(ap("NB", 192, 256), [[15, 64]], 63, 0)
+    ts(ap("NB", 0, 64), ap("NB", 192, 256), ap("MK", 0, 1), A.mult)
+    tt(ap("NB", 0, 64), ap("NB", 128, 192), ap("NB", 0, 64), A.subtract)
+    ts(ap("NBh", 0, 64), ap("NB", 0, 64), ap("col", 0, 1), A.add)
+    ts(ap("NB", 64, 128), ap("NB", 192, 256), ap("MK", 0, 1), A.mult, 2.0, A.add)
+    ts(ap("NB", 128, 192), ap("NB", 192, 256), -1.0, A.mult, 1071.0, A.add)
+    ts(ap("NB", 128, 192), ap("NB", 128, 192), ap("MK", 15, 16), A.mult)
+    tt(ap("NB", 64, 128), ap("NB", 64, 128), ap("NB", 128, 192), A.add)
+    EQ, EQ1, L4, M4, IR, WK, WK2 = [ap("q4", 64 * i, 64 * i + 64) for i in range(7)]
+    n15, m15 = ap("col", 2, 3), ap("MK", 15, 16)
+    tt(EQ, ap("IF", 0, 64), ap("IF", 64, 128), A.add)
+    tt(EQ1, ap("SH", 384, 448), ap("SH", 448, 512), A.add)
+    tt(L4, ap("LT", 0, 64), ap("LT", 64, 128), A.add)
+    tt(M4, ap("BO", 0, 64), ap("BO", 64, 128), A.add)
+    iota(IR, [[0, 4], [1, 16]], 0, 0)
+    tt(IR, IR, M4, A.mult)
+    ts(ap("WC", 0, 64), EQ, 2.0 ** -18, A.mult)
+    ts(ap("WC", 64, 128), EQ1, 2.0 ** -18, A.mult)
+    ts(ap("WH", 0, 64), EQ, 2.0 ** -26, A.mult)
+    ts(ap("WH", 64, 128), L4, 2.0 ** -19, A.mult)
+    ts(ap("WL", 128, 192), L4, 2.0 ** -19, A.mult)
+    ts(ap("WH", 128, 192), IR, 128.0, A.mult, n15, A.mult)
+    ms(ap("WH", 143, 192, 16), 0.0)
+    cp(ap("WL", 192, 256), ap("WH", 128, 192))
+    ts(ap("WL", 64, 128), IR, 0.125, A.mult, m15, A.mult)
+    ts(WK, EQ, 2.0 ** -19, A.mult, n15, A.mult)
+    tt(ap("WL", 0, 64), WK, ap("WL", 64, 128), A.add)
+    ts(WK, M4, 4.0, A.mult, m15, A.mult)
+    ts(WK2, L4, -1920.0, A.mult)
+    tt(WK, WK, WK2, A.add)
+    ts(WK2, M4, 128.0, A.mult, n15, A.mult)
+    for k in range(14):
+        tt(ap("WZ", 64 * k, 64 * k + 64), WK if k == 0 else ap("WZ", 64 * k - 64, 64 * k), WK2, A.add)
+
+    Xw, Gw = ap("X", 0, W), ap("G", 0, W)
+    for c in range(NCH):
+        cur[0] = c
+        s = str(c)
+
+        def a_(n, c0, c1, st=1, p0=0, p1=128):
+            return ap(n + s, c0, c1, st, p0, p1)
+
+        def sh(i, n=1):
+            return a_("sh", 64 * i, 64 * (i + n))
+
+        def sf(i, n=1):
+            return a_("sf", 64 * i, 64 * (i + n))
+
+        def si(i, n=1):
+            return a_("si", 64 * i, 64 * (i + n))
+        av, bv, lv = a_("abl", 0, 64), a_("abl", 64, 128), a_("abl", 128, 192)
+        for n in ("xa", "xu", "lp"):
+            ms(a_(n, 1024, 1040), 0.0)
+        ms(a_("bd", 0, 512), 0.0)
+        for k in (0, 15):
+            ms(ap3("so" + s, 14, 192, 16, k, k + 1), 0.0)
+            ms(ap3("so" + s, 78, 128, 16, k, k + 1), 2.0 ** -26)
+        for q in range(2):
+            cp(a_("oab", 64 * q, 64 * q + 64), ap("lin", 128 * q + 64 * c, 128 * q + 64 * c + 64))
+        for q in range(3):
+            cp(a_("abl", 64 * q, 64 * q + 64), ap("lin", 128 * q + 64 * c, 128 * q + 64 * c + 64))
+        for r in range(RO):
+            u = s + str(r)
+
+            def ps(n, c0, c1, st=1, p0=0, p1=128):
+                return ap("ps:" + n + u, c0, c1, st, p0, p1)
+            Rw, Sd = "R" + u, "S" + u
+            m8, m0, sg, dif, md8, md0, l8 = sh(0), sh(1), sh(2), sh(3), sh(4), sh(5), sh(6)
+            for h in range(2):
+                o = 512 * h
+                act(a_("xa", o, o + 512), ind(Xw, a_("oab", 32 * h, 32 * h + 32)))
+                if h < opt["d_act"]:
+                    act(a_("ad", o, o + 512), ind(Xw, a_("oab", 64 + 32 * h, 96 + 32 * h)))
+                    mm(grp(ps("dd%d" % h, 0, 512), [(I1, a_("ad", o, o + 512)), (IN, a_("xa", o, o + 512))]))
+                    act(a_("d", o, o + 512), ps("dd%d" % h, 0, 512))
+                else:
+                    tt(a_("d", o, o + 512), ind(Xw, a_("oab", 64 + 32 * h, 96 + 32 * h)), a_("xa", o, o + 512), A.subtract)
+            for h in range(2):
+                mm([(ps("L%d" % h, j, 512, 8), ap("BC", 128 * (2 * j + h), 128 * (2 * j + h) + 128), lv, True, True)
+                    for j in range(8)])
+                if opt["dg_act"] and opt["ls_first"]:
+                    act(a_("Ls", h, 1024, 2), ps("L%d" % h, 0, 512))
+                tt(a_("ld", h, 1024, 2), a_("d", h, 1024, 2), ps("L%d" % h, 0, 512), A.mult)
+                if opt["dg_act"] and not opt["ls_first"]:
+                    act(a_("Ls", h, 1024, 2), ps("L%d" % h, 0, 512))
+            late = r == 0 or not opt["early"]
+            for h in range(2):
+                mm([(ps("R%d" % h, 0, 512), I8, a_("xa", h, 1024, 2), True, False),
+                    (ps("R%d" % h, 0, 512), I1, a_("ld", h, 1024, 2), False, not (opt["t_act"] and opt["racc"]))])
+                if late:
+                    act(ap(Sd, 128 * h, 128 * h + 64), ps("R%d" % h, 7 * h, 512, 8))
+                act(ap(Rw, 128 + h, 1152, 2), ps("R%d" % h, 0, 512))
+                if not opt["t_act"]:
+                    act(a_("ad", h, 1024, 2), ps("R%d" % h, 0, 512))
+            act(m8, lv, F.Relu, 1.0, -7.0)
+            act(m0, lv, F.Relu, -1.0, 1.0)
+            act(sh(8), lv, F.Relu, 8.0, -56.0)
+            tt(sh(7), lv, sh(8), A.subtract)
+            lin(l8, sh(7), -1.0, 8.0)
+            tt(dif, bv, av, A.subtract)
+            tt(md8, m8, dif, A.mult)
+            tt(md0, m0, dif, A.mult)
+            IK = ap("ID", 640, 768)
+            mm(grp(ps("ls", 0, 64), [(I1, av), (I1, md8)]) + grp(ps("ls", 64, 128), [(I1, bv), (IK, m8), (IK, m0), (IN, md0)]))
+            cp(a_("oen", 0, 128), ps("ls", 0, 128))
+            for q in range(2):
+                act(a_("en", 1024 * q, 1024 * q + 1024), ind(ap("EN", 0, 2 * W), a_("oen", 64 * q, 64 * q + 64)))
+            for q in range(2):
+                mm(grp(ps("E", 64 * q, 64 * q + 64),
+                       [(ap("UE", 15 - k, 143 - k), a_("en", 1024 * q + k, 1024 * q + 1024, 16)) for k in range(16)]))
+            tt(sf(0, 2), ps("E", 0, 128), sh(6, 2), A.mult)
+            def send(v):
+                add("Q", [("xfer", (ap("R" + v, 0, 128), ap("S" + v, 0, 192), v)), ("none", (ap("R" + v, 1152, 1280),))],
+                    1000, sem="h" + v, lat=opt["lat"], ch=c)
+            if late:
+                tt(ap(Sd, 64, 128), sf(0), sf(1), A.add)
+                send(u)
+                et = [(ap("SH", 0, 128), ap(Sd, 64, 128))]
+            else:
+                et = [(ap("SH", 0, 128), sf(0)), (ap("SH", 0, 128), sf(1))]
+            mm(grp(ps("N", 0, 64),
+                   [(ap("DG", 128 * k, 128 * k + 128), a_("en", 1024 + k, 2048, 16)) for k in range(16)]))
+            nma, sg = sh(11), si(0)
+            tt(nma, ps("N", 0, 64), av, A.subtract)
+            ts(sg, lv, 1.0 / 7, A.mult, -4.0 / 7, A.add)
+            for h in range(2):
+                o = 64 * h
+                act(a_("bd", 384 + o, 448 + o, 1, o, o + 64), a_("abl", 0, 64, 1, o, o + 64))
+            act(a_("ga", 0, 1024), ind(Gw, a_("oab", 0, 64)))
+            if opt["dg_act"]:
+                act(a_("gb", 0, 1024), ind(Gw, a_("oab", 64, 128)))
+                for h in range(2):
+                    mm(grp(ps("dg%d" % h, 0, 512), [(I1, a_("gb", h, 1024, 2)), (IN, a_("ga", h, 1024, 2))]))
+                    tt(a_("lg", h, 1024, 2), a_("Ls", h, 1024, 2), ps("dg%d" % h, 0, 512), A.mult)
+            else:
+                tt(a_("gb", 0, 1024), ind(Gw, a_("oab", 64, 128)), a_("ga", 0, 1024), A.subtract)
+                for h in range(2):
+                    tt(a_("lg", h, 1024, 2), a_("gb", h, 1024, 2), ps("L%d" % h, 0, 512), A.mult)
+            mm(grp(ps("ed", 0, 64), et + [(ap("SH", 128, 256), ap(Rw, 0, 64)), (ap("SH", 256, 384), ap(Rw, 1216, 1280))]))
+            ts(sf(2), ps("ed", 0, 64), 0.0, A.is_ge)
+            tt(sh(2), sf(2), ap("NB", 64, 128), A.mult)
+            mm(grp(ps("ed", 64, 128), [(I1, ap("NBh", 0, 64)), (I1, sh(2))]))
+            cp(a_("ot", 0, 64), ps("ed", 64, 128))
+            for h in range(2):
+                o = 512 * h
+                if opt["t_act"]:
+                    act(a_("t", o, o + 512), ind(ap(Rw, 64, 1216), a_("ot", 32 * h, 32 * h + 32)))
+                else:
+                    tt(a_("t", o, o + 512), ind(ap(Rw, 64, 1216), a_("ot", 32 * h, 32 * h + 32)), a_("ad", o, o + 512),
+                       A.subtract)
+            for h in range(2 if opt["t_act"] else 0):
+                mm(grp(ps("g%d" % h, 0, 512), [(I8, a_("ga", h, 1024, 2)), (I1, a_("lg", h, 1024, 2))]))
+                act(a_("ad", h, 1024, 2), ps("g%d" % h, 0, 512))
+                tt(a_("PA", h, 1024, 2), a_("d", h, 1024, 2), ps("g%d" % h, 0, 512), A.mult)
+                gr = grp(ps("t%d" % h, 0, 512), [(ap("ID", 768, 896), a_("xa", h, 1024, 2)), (IN, a_("ld", h, 1024, 2)),
+                                                 (I1, a_("t", h, 1024, 2))])
+                if opt["racc"]:
+                    tp = ps("R%d" % h, 0, 512)
+                    mm([(tp, IN, a_("t", h, 1024, 2), False, True)])
+                else:
+                    tp = ps("t%d" % h, 0, 512)
+                    mm(gr[:2])
+                    ops[-1]["after"] = a_("ot", 0, 64)
+                    mm(gr[2:])
+                tt(a_("PA", 1024 + h, 2048, 2), a_("ad", h, 1024, 2), tp, A.mult)
+                tt(a_("PB", 1024 + h, 2048, 2), a_("d", h, 1024, 2), tp, A.mult)
+                act(a_("PB", h, 1024, 2), tp, F.Square)
+            for h in range(0 if opt["t_act"] else 2):
+                mm(grp(ps("g%d" % h, 0, 512), [(I8, a_("ga", h, 1024, 2)), (I1, a_("lg", h, 1024, 2))]))
+                ops[-1]["after"] = a_("ot", 0, 64)
+                tt(a_("PA", h, 1024, 2), a_("d", h, 1024, 2), ps("g%d" % h, 0, 512), A.mult)
+                tt(a_("PA", 1024 + h, 2048, 2), a_("t", h, 1024, 2), ps("g%d" % h, 0, 512), A.mult)
+                act(a_("PB", h, 1024, 2), a_("t", h, 1024, 2), F.Square)
+                mm([(ps("d%d" % h, 0, 512), I1, a_("d", h, 1024, 2), True, True)])
+                ops[-1]["after"] = a_("ot", 0, 64)
+                tt(a_("PB", 1024 + h, 2048, 2), a_("t", h, 1024, 2), ps("d%d" % h, 0, 512), A.mult)
+            for h in range(2):
+                for n in ("PB", "PA"):
+                    mm([(ps("s" + n, k, 128, 16), a_(n, k, 2048, 16), ap("BO8", 0, 8), True, True) for k in range(h, 16, 2)])
+            act(sf(4, 2), ps("sPB", 0, 128))
+            tt(sf(4, 2), sf(4, 2), ps("sPA", 0, 128), A.mult)
+            mm([(ps("df", 0, 64), sf(4, 2), ap("PMI", 0, 64), True, True)])
+            pas, dl, l1, uu, lA, lB = sh(13), sh(14), sh(15), sh(16), sh(17), sh(18)
+            pn, pQ, pQ2, psg = [a_("nw", 0, 64), a_("nw", 64, 128), a_("nw", 128, 192), sh(19)]
+            tt(sf(3), ps("df", 0, 64), sg, A.mult)
+            ts(dl, ps("df", 0, 64), -1.0, A.max, 1.0, A.min)
+            ts(pas, sf(3), 0.0, A.max, 1.0, A.min)
+            tt(l1, lv, dl, A.add)
+            tt(pn, pas, nma, A.mult)
+            mm(grp(ps("uu", 0, 64), [(I1, av), (I1, pn)]))
+            cp(a_("ou", 0, 64), ps("uu", 0, 64))
+            ts(lA, l1, 0.0, A.max, -8.0, A.add)
+            act(lB, lA, F.Abs)
+            act(lA, lB, F.Identity, -1.0, 8.0)
+            tt(pQ, pas, dif, A.mult)
+            tt(pQ2, m8, pn, A.mult)
+            tt(sh(12), m8, pQ, A.mult)
+            ts(psg, l1, 0.0, A.max, 8.0, A.min)
+            ts(dl, l1, 4.5, A.is_gt)
+            for h in range(2):
+                tt(a_("bd", 64 * h, 64 * h + 64, 1, 64 * h, 64 * h + 64), a_("sh", 896, 960, 1, 64 * h, 64 * h + 64),
+                   a_("sh", 192, 256, 1, 64 * h, 64 * h + 64), A.mult)
+            act(a_("xu", 0, 1024), ind(Xw, a_("ou", 0, 64)))
+            for h in range(2):
+                mm([(ps("M%d" % h, j, 512, 8), ap("BC", 128 * (2 * j + h), 128 * (2 * j + h) + 128), lA, True, True)
+                    for j in range(8)])
+                tt(a_("lp", h, 1024, 2), a_("d", h, 1024, 2), ps("M%d" % h, 0, 512), A.mult)
+            M1, MN, M8, MN7, MH = [ap("MD", 128 * i, 128 * i + 128) for i in range(5)]
+
+            mm(grp(ps("nd", 0, 64), [(M1, av), (M1, pn), (MN, pQ2), (M1, sh(12))]) +
+               grp(ps("nd", 64, 128), [(M1, bv), (M1, pQ2), (MN, pQ)]) + grp(ps("nd", 128, 192), [(MN7, l1), (M8, psg)]))
+            act(a_("eb", 0, 192), ps("nd", 0, 192))
+            early = opt["early"] and r < RO - 1
+            if early:
+                Sn = "S" + s + str(r + 1)
+                lin(a_("eb", 192, 256), a_("eb", 128, 192), -1.0, 8.0)
+                mm(grp(ps("el", 0, 16), [(ap("VE", 15 - 4 * j - q, 143 - 4 * j - q), a_("eb", 64 * q + 16 * j, 64 * q + 16 * j + 16))
+                                         for j in range(4) for q in range(2)]))
+                cp(a_("oe", 0, 16), ps("el", 0, 16))
+                act(a_("ee", 0, 256), ind(ap("EN", 0, W), a_("oe", 0, 16)))
+                gr = []
+                for q in range(2):
+                    for j in range(4):
+                        gr += grp(ps("eE", 64 * (1 - q) + 16 * j, 64 * (1 - q) + 16 * j + 16),
+                                  [(ap("UE", 15, 143), a_("ee", 4 * j + q, 256, 16)), (ap("UE", 0, 128), a_("ee", 4 * j + q + 2, 256, 16))])
+                mm(gr)
+                tt(sf(10, 2), ps("eE", 0, 128), a_("eb", 128, 256), A.mult)
+                tt(ap(Sn, 64, 128), sf(10), sf(11), A.add)
+                gr = []
+                for h in range(2):
+                    gr += grp(ps("eR", 64 * h, 64 * h + 64), [(I7, a_("xa", 15 * h, 1024, 16)), (I1, a_("lp", 15 * h, 1024, 16)),
+                                                              (I1, a_("xu", 15 * h, 1024, 16))])
+                mm(gr)
+                for h in range(2):
+                    act(ap(Sn, 128 * h, 128 * h + 64), ps("eR", 64 * h, 64 * h + 64))
+                send(s + str(r + 1))
+            for h in range(2):
+                gr = grp(ps("D%d" % h, 0, 512),
+                         [(I7, a_("xa", h + 1, 1025, 2)), (IN7, a_("xa", h, 1024, 2)), (I1, a_("lp", h + 1, 1025, 2)),
+                          (IN, a_("lp", h, 1024, 2)), (I1, a_("xu", h + 1, 1025, 2)), (IN, a_("xu", h, 1024, 2))])
+                mm(gr[:2])
+                ops[-1]["after"] = a_("ou", 0, 64)
+                mm(gr[2:4])
+                mm(gr[4:])
+                act(a_("ad", h, 1024, 2), ps("D%d" % h, 0, 512), F.Abs)
+            gr = grp(ps("H", 0, 64), [(ap("UH", 15 - j, 143 - j), a_("ad", j, 1024, 16)) for j in range(0, 15, 2)] +
+                     [(ap("UH", 0, 128), ap("ONE", 0, 64))] +
+                     [(ap("UH", 15 - j, 143 - j), a_("ad", j, 1024, 16)) for j in range(1, 15, 2)])
+            mm(gr[:9])
+            mm(gr[9:])
+            for h in range(2):
+                o = 64 * h
+                ts(a_("bd", 128 + o, 192 + o, 1, o, o + 64), ps("H", 0, 64, 1, o, o + 64), MAGIC, A.add, -MAGIC, A.add)
+            for h in range(2):
+                o = 64 * h
+                tt(a_("bd", 256 + o, 320 + o, 1, o, o + 64), ps("H", 0, 64, 1, o, o + 64),
+                   a_("bd", 128 + o, 192 + o, 1, o, o + 64), A.subtract)
+            cb, hb, lb = a_("bd", 0, 128), a_("bd", 128, 256), a_("bd", 256, 384)
+            ab = a_("bd", 384, 512)
+            mm(grp(ps("py", 0, 64), [(cb, ap("WC", 0, 64)), (ab, ap("WC", 0, 64)), (lb, ap("WL", 0, 64))]) +
+               grp(ps("py", 64, 128), [(cb, ap("WC", 64, 128)), (ab, ap("WC", 64, 128)), (lb, ap("WL", 64, 128)),
+                                       (hb, ap("WH", 0, 64))]) +
+               grp(ps("py", 128, 256), [(lb, ap("WL", 128, 256)), (hb, ap("WH", 64, 192))]))
+            act(a_("pay", 0, 256), ps("py", 0, 256))
+            for h in range(2):
+                wz = ap("WZ", 448 * h, 448 * h + 448)
+                mm(grp(ps("Z%d" % h, 0, 448), [(hb, wz), (lb, wz)]))
+                for q in range(3):
+                    add("V", [("scan", (ap3("so" + s, 64 * q, 64 * q + 64, 1, 1 + 7 * h + j, 2 + 7 * h + j),
+                                        ps("Z%d" % h, 64 * j, 64 * j + 64), a_("pay", 64 * q, 64 * q + 64)))
+                              for j in range(7)], 7 * 64 * cy, ch=c)
+            gp, rc, y, x = sf(6), sf(7), sf(8), sf(9)
+            ts(si(0, 2), ap3("so" + s, 14, 128, 16, 0, 16), 2.0 ** 26, A.mult, 64.0, A.add)
+            lin(y, ap3("so" + s, 142, 192, 16, 0, 16), -15.0 * 2.0 ** 26, 0.0)
+            ts(si(4, 2), si(0, 2), 255, A.bitwise_and)
+            ts(si(2, 2), si(0, 2), 8, A.logical_shift_right, 2047, A.bitwise_and)
+            tt(y, y, a_("pay", 192, 256), A.add)
+            lin(gp, si(5), 128.0, -8256.0)
+            tt(gp, gp, si(4), A.add)
+            ts(gp, gp, 15.0, A.mult, 1.0 / 32, A.max)
+            add("V", [("rcp", (rc, gp))], 190 + 6 * 64 * cy, ch=c)
+            lin(y, y, 8.0, 0.25)
+            act(sh(8, 2), si(2, 2))
+            tt(x, y, rc, A.mult)
+            ts(sh(13), x, 1023.97, A.add)
+            ts(sh(10), sh(13), -1023.5, A.add)
+            tt(x, sh(10), gp, A.mult)
+            tt(sh(13), x, y, A.is_le)
+            st = []
+            for q, src in ((0, [8]), (1, [9]), (2, [10, 13])):
+                for h in range(2):
+                    o = 64 * h
+                    st += grp(ps("st", 64 * q, 64 * q + 64, 1, o, o + 64),
+                              [(ap("ID", o, o + 64), a_("eb", 64 * q, 64 * q + 64))] +
+                              ([(ap("MD", 512 + o, 576 + o), ap("ONE", 0, 64))] if q == 2 else []) +
+                              [(a_("sh", 64 * x, 64 * x + 64, 1, o, o + 64), ap("ID", o, o + 64, 1, o, o + 64)) for x in src])
+            mm(st[:8])
+            mm(st[8:])
+            if r < RO - 1:
+                cp(a_("oab", 0, 128), ps("st", 0, 128))
+                act(a_("abl", 0, 192), ps("st", 0, 192))
+            else:
+                act(a_("res", 0, 192), ps("st", 0, 192))
+                for q, n in enumerate(("ya", "yb", "yl")):
+                    dma("S" if q == 1 else "Y", "o%d%d" % (c, q), (n, 64 * c), a_("res", 64 * q, 64 * q + 64), 2000)
+    return ops
+
+
+def schedule(ops, opt):
+    hist = {}
+    for op in ops:
+        dep = set()
+        acc = [(a, False) for a in op["rd"]] + [(a, True) for a in op["wr"]]
+        if "after" in op:
+            acc.append((op["after"], False))
+        for a, w in acc:
+            if a["n"] == "hbm":
+                continue
+            isps = a["n"][:3] == "ps:"
+            for (o2, a2, w2) in hist.get(a["n"], ()):
+                if o2 is op:
+                    continue
+                if isps and o2["e"] != op["e"]:
+                    dep.add(o2["id"])
+                elif (w or w2) and a["m"] & a2["m"] and a["p"][0] < a2["p"][1] and a2["p"][0] < a["p"][1]:
+                    if "nowaw" in a and "nowaw" in a2:
+                        continue
+                    dep.add(o2["id"])
+        for a, w in acc:
+            hist.setdefault(a["n"], []).append((op, a, w))
+        op["dep"] = dep
+        op["tiles"] = set(a["n"] for a, w in acc if a["n"][:3] == "ps:")
+    users = {}
+    for op in ops:
+        for t in op["tiles"]:
+            users.setdefault(t, []).append(op["id"])
+    succ = [[] for o in ops]
+    for op in ops:
+        for d in op["dep"]:
+            succ[d].append(op["id"])
+    X, SAME = 120.0, 80.0
+    for op in reversed(ops):
+        op["pr"] = op["c"] + op.get("lat", 0) + max([ops[s]["pr"] + X for s in succ[op["id"]]] + [0])
+    free = dict((e, 0.0) for e in "VSPQY")
+    left = [len(o["dep"]) for o in ops]
+    ready = [o["id"] for o in ops if not o["dep"]]
+    bank_of, tenant, order = {}, [None] * 8, []
+    done = set()
+
+    def avail(op, extra=()):
+        t = 0.0
+        for d in list(op["dep"]) + list(extra):
+            o = ops[d]
+            t = max(t, o["end"] + (0 if o["e"] == op["e"] == "P" else SAME if o["e"] == op["e"] and "lat" not in o else X))
+        return t
+    base = np.array([op["pr"] for op in ops])
+    chs = np.array([op["ch"] for op in ops])
+    pr = base + opt["bias"] * (chs == 0)
+    for seed in opt["steps"]:
+        rs = np.random.RandomState(seed)
+        mid, wid, amp = rs.rand() * base.max(), 300 + rs.rand() ** 2 * 8000, rs.randn() * 2500
+        pr = pr + amp * ((np.abs(base - mid) < wid) & (chs == rs.randint(NCH)) & (rs.rand(len(ops)) < rs.choice([0.3, 1.0])))
+    pr = [float(x) for x in pr]
+
+    def gap(a, b):
+        return a.get("lat", 0) + (0 if a["e"] == b["e"] == "P" else SAME if a["e"] == b["e"] and "lat" not in a else X)
+    fw = [[(d, gap(ops[d], op)) for d in op["dep"]] for op in ops]
+    bw = [[(s, gap(op, ops[s])) for s in succ[op["id"]]] for op in ops]
+
+    def serial(key, pre, post, tail):
+        busy = dict((e, []) for e in "VSPQY")
+        n = [len(x) for x in pre]
+        rdy = [(key[i], i) for i in range(len(ops)) if not n[i]]
+        end = [0.0] * len(ops)
+        while rdy:
+            j = min(rdy)
+            rdy.remove(j)
+            i = j[1]
+            t = max([end[d] + g for d, g in pre[i]] + [ops[i].get("lat", 0) if tail else 0])
+            c, b = ops[i]["c"], busy[ops[i]["e"]]
+            k = len(b)
+            while k > 0 and b[k - 1][1] > t:
+                k -= 1
+            while k < len(b) and b[k][0] < t + c:
+                t = max(t, b[k][1])
+                k += 1
+            b.insert(k, (t, t + c))
+            end[i] = t + c
+            for s, g in post[i]:
+                n[s] -= 1
+                if not n[s]:
+                    rdy.append((key[s], s))
+        return end
+    if opt["fbi"]:
+        key = [-x for x in pr]
+        for it in range(opt["fbi"]):
+            e1 = serial(key, fw, bw, False)
+            e2 = serial([-x for x in e1], bw, fw, True)
+            key = [-x for x in e2]
+        e1 = serial(key, fw, bw, False)
+        top = max(e2)
+        pr = [-(e1[i] - ops[i]["c"]) * (1 - opt["mix"]) - (top - e2[i]) * opt["mix"] for i in range(len(ops))]
+    while ready:
+        cand = []
+        for i in ready:
+            op = ops[i]
+            new = [t for t in op["tiles"] if t not in bank_of]
+            extra, pick = [], None
+            if new:
+                cands = [b for b in range(8) if tenant[b] is None or all(x in done for x in users[tenant[b]])]
+                if not cands:
+                    continue
+                pick = min(cands, key=lambda b: 0 if tenant[b] is None else max(ops[x]["end"] for x in users[tenant[b]]))
+                extra = [x for x in users[tenant[pick]]] if tenant[pick] else []
+            st = max(free[op["e"]], avail(op, extra))
+            cand.append((st, i, op, new, pick, extra))
+        first = min(cand, key=lambda x: x[:2])
+        lim = first[0] + opt["th"] * first[2]["c"] + 30
+        if opt["th"] < 0:
+            st, i, op, new, pick, extra = max(cand, key=lambda x: (pr[x[1]], -x[1]))
+        else:
+            st, i, op, new, pick, extra = max([x for x in cand if x[2]["e"] == first[2]["e"] and x[0] <= lim],
+                                              key=lambda x: (pr[x[1]], -x[1]))
+        if new:
+            bank_of[new[0]] = pick
+            tenant[pick] = new[0]
+            op["dep"] = op["dep"] | set(extra)
+        op["st"] = st
+        free[op["e"]] = st + op["c"]
+        op["end"] = st + op["c"] + op.get("lat", 0)
+        order.append(op)
+        done.add(op["id"])
+        ready.remove(op["id"])
+        for s in succ[op["id"]]:
+            left[s] -= 1
+            if left[s] == 0:
+                ready.append(s)
+    cnt = dict((e, 0) for e in "VSPQ")
+    for op in order:
+        if "sem" not in op:
+            cnt[op["e"]] += 1
+            op["sig"] = (op["e"], cnt[op["e"]])
+        else:
+            op["sig"] = (op["sem"], 16)
+    seen = dict((e, {}) for e in "VSPQY")
+    for op in order:
+        need = {}
+        for d in op["dep"]:
+            s, v = ops[d]["sig"]
+            if ops[d]["e"] == "P" and op["e"] == "P":
+                continue
+            need[s] = max(need.get(s, 0), v)
+        op["waits"] = [(s, v) for s, v in need.items() if seen[op["e"]].get(s, 0) < v]
+        for s, v in op["waits"]:
+            seen[op["e"]][s] = v
+    return order, bank_of, cnt
+
+
+PLAN = {}
+
+
+def plan():
+    if not PLAN:
+        ops = build(OPT)
+        PLAN["p"] = schedule(ops, OPT)
+    return PLAN["p"]
+
+
+def helper_of(src, dst, T, topo):
+    if topo.may_write(src, dst):
+        return dst
+    c = [x for x in topo.cores_of(src) if T.rank_of(x) is None and topo.may_write(x, dst)]
+    c.sort(key=lambda x: topo.die(x) != topo.die(src))
+    return c[0]
+
+
+def bits(engines):
+    m = 0
+    for e in engines:
+        m |= 1 << e
+    return m
+
+
+def rank_program(g, core, T, topo):
+    order, bank_of, cnt = plan()
+    n = len(T.cores)
+    msgs = [op["ins"][0][1][2] for op in order if op["ins"][0][0] == "xfer"]
+    rank = T.rank_of(core)
+    if rank is None:
+        for r in range(n):
+            for side, (lo, hi) in ((-1, (1152, 1280)), (1, (0, 128))):
+                src, dst = T.cores[r], T.cores[(r + side) % n]
+                if helper_of(src, dst, T, topo) != core:
+                    continue
+                rid, pid = topo.addr(dst, core)
+                eng = topo.engines(core, dst)[:8]
+                for u in msgs:
+                    g.wait_ge(T.sem["h" + u], 8)
+                    buf = T["R" + u][:, lo:hi]
+                    g.remote_dma(buf, buf, T.sem["h" + u], T.sem.sent, pid, rid, bits(eng))
+                g.wait_ge(T.sem.sent, len(eng) * len(msgs))
+        return
+    Q = {"V": g.vector, "S": g.scalar, "P": g.tensor, "Q": g, "Y": g.sync}
+
+    def real(a):
+        if not isinstance(a, dict):
+            return a
+        if "win" in a:
+            return real(a["win"]).indirect(real(a["off"]))
+        nm = a["n"]
+        if nm[:3] == "ps:":
+            nm = "bank%d" % bank_of[nm]
+        return T[nm][a["i"]]
+    for op in order:
+        q = Q[op["e"]]
+        for s, v in op["waits"]:
+            q.wait_ge(T.sem[s], v)
+        last = None
+        for kind, args in op["ins"]:
+            if kind == "xfer":
+                u = args[2]
+                tr, used = [], []
+                for side, (lo, hi), s0 in ((-1, (1152, 1280), 0), (1, (0, 128), 64)):
+                    to = helper_of(core, T.cores[(rank + side) % n], T, topo)
+                    eng = [e for e in topo.engines(core, to) if e not in used][:8]
+                    used.extend(eng)
+                    rid, pid = topo.addr(to, core)
+                    tr.append(RemoteDMATransfer(dst_ids=[DstId(rid=rid, pnc=pid)], dma_engine_mask=bits(eng),
+                                                remote_sem=T.sem["h" + u], src=T["S" + u][:, s0:s0 + 128],
+                                                dst=T["R" + u][:, lo:hi]))
+                g.remote_dma_fused(tr, local_sem=T.sem.sent)
+                continue
+            if kind == "none":
+                continue
+            if kind == "dma":
+                o, i = args[2]
+                o = real(o) if isinstance(o, dict) else T[o[0]][:, o[1]:o[1] + 64]
+                i = real(i) if isinstance(i, dict) else T[i[0]][:]
+                q.dma_start(o, i).then_inc(T.sem[op["sem"]], 16)
+                continue
+            a = [real(x) for x in args]
+            if kind == "tt":
+                last = q.tensor_tensor(a[0], a[1], a[2], a[3])
+            elif kind == "ts":
+                last = q.tensor_scalar(*(a if a[5] is not None else a[:5]))
+            elif kind == "cp":
+                last = q.tensor_copy(a[0], a[1])
+            elif kind == "ms":
+                last = q.memset(a[0], a[1])
+            elif kind == "rcp":
+                last = q.reciprocal(a[0], a[1])
+            elif kind == "scan":
+                last = q.tensor_tensor_scan(a[0], a[1], a[2], 0.0, A.max, A.min)
+            elif kind == "act":
+                last = q.activation(a[0], a[1], a[2], bias=a[3], scale=a[4])
+            elif kind == "mm":
+                last = q.matmul(a[0], a[1], a[2], a[3], a[4])
+            elif kind == "sel":
+                last = q.affine_select(*a)
+            elif kind == "iota":
+                if SCRATCH[args[0]["n"]][2] == I32:
+                    last = q.iota(*a)
+                else:
+                    last = q.iota(a[0], a[1], a[2], a[3], allow_small_or_imprecise_dtypes=True)
+        if last is not None:
+            last.then_inc(T.sem[op["e"]], 1)
+    for e in "VSPQ":
+        g.wait_ge(T.sem[e], cnt[e])
+    for s in DMAS:
+        g.wait_ge(T.sem[s], 16)
+    for u in msgs:
+        g.wait_ge(T.sem["h" + u], 16)
+    g.wait_ge(T.sem.sent, 16 * len(msgs))

@@ -1,3 +1,4 @@
+import math
 import numpy as np
 from concourse.bass import DstId, RemoteDMATransfer
 from concourse.mybir import dt, AluOpType, AxisListType, ActivationFunctionType
@@ -7,35 +8,35 @@ F = ActivationFunctionType
 W, RO, NCH = 1536, 3, 2
 H16, B16, F32, I32, U16 = "float16", "bfloat16", "float32", "int32", "uint16"
 MAGIC = 1.5 * 2.0 ** 23
-OPT = {"dg_act": False, "gam": 1.56, "pe": 0.42, "lat": 4500.0, "bias": 4000.0, "act_small": True,
-       "ttg": 0.0, "early": True, "d_act": 0, "t_act": False, "racc": False, "ls_first": False, "th": 0.0, "fbi": 1, "mix": 0.0,
-       "steps": [95816, 31019, 44295, 43595, 72084, 21418, 60966, 94642, 27383, 91537, 87538, 40321, 67301, 11044, 59118, 24142,
-                 23150, 40506, 69720, 71307, 72656, 68659, 90942, 89358, 9372, 9289, 28749, 60054, 26098, 60321, 92555,
-                 30369, 38492, 73172, 85073, 23366, 54715, 49595, 18069, 1629, 72566]}
-REF = {"gam": 1.56, "pe": 0.42, "lat": 4500.0, "ttg": 0.0}
+OPT = {"gam": 1.56, "pe": 0.42, "lat": 6500.0, "bias": 3000.0, "th": 0.0, "X": 300.0, "same": 150.0, "en": "SS",
+       "tries": 22000, "seed": 1, "hot": 500.0, "cold": 20.0,
+       "pa": "VS", "rc": "SS", "d": "QQ", "dl": "VVVV", "u16": "S", "cvt": "V", "eng": 8,
+       "g": "VV", "nq": 4, "st2": True, "py2": True, "clock": True}
 
 SCRATCH = {
     "X": ("sbuf", [128, W], B16), "G": ("sbuf", [128, W], B16), "EN": ("sbuf", [128, 2 * W], I32),
-    "e96": ("sbuf", [128, 96], I32), "ehl": ("sbuf", [128, 192], I32), "lin": ("sbuf", [128, 384], I32),
+    "PK": ("sbuf", [128, W], F32),
+    "e96": ("sbuf", [128, 96], I32), "ehl": ("sbuf", [128, 192], I32), "lin": ("sbuf", [128, 2, 192], I32),
     "BO": ("sbuf", [128, 128], F32), "IF": ("sbuf", [128, 128], F32), "SH": ("sbuf", [128, 512], F32),
-    "LT": ("sbuf", [128, 128], F32), "BOh": ("sbuf", [128, 128], H16),
-    "ID": ("sbuf", [128, 896], H16), "BC": ("sbuf", [128, 2048], H16), "DG": ("sbuf", [128, 2048], H16),
-    "MD": ("sbuf", [128, 640], H16), "UH": ("sbuf", [128, 144], H16), "UE": ("sbuf", [128, 144], H16),
-    "BO8": ("sbuf", [128, 8], F32), "PMI": ("sbuf", [128, 64], F32), "ONE": ("sbuf", [128, 64], H16),
+    "LT": ("sbuf", [128, 128], F32), "BOh": ("sbuf", [128, 128], B16),
+    "ID": ("sbuf", [128, 896], H16), "BC": ("sbuf", [128, 2048], B16), "DG": ("sbuf", [128, 2048], B16),
+    "MD": ("sbuf", [128, 256], H16), "UH": ("sbuf", [128, 144], H16), "UE": ("sbuf", [128, 432], H16),
+    "BO8": ("sbuf", [128, 8], F32), "PMI": ("sbuf", [128, 128], F32), "ONE": ("sbuf", [128, 128], H16),
     "pi": ("sbuf", [128, 8], I32), "col": ("sbuf", [128, 16], F32), "MK": ("sbuf", [128, 32], F32),
     "q4": ("sbuf", [128, 512], F32), "WZ": ("sbuf", [128, 896], H16),
     "WC": ("sbuf", [128, 128], B16), "WH": ("sbuf", [128, 192], B16), "WL": ("sbuf", [128, 256], B16),
-    "NB": ("sbuf", [128, 256], F32), "VE": ("sbuf", [128, 144], H16), "NBh": ("sbuf", [128, 64], H16),
+    "NB": ("sbuf", [128, 320], F32), "VE": ("sbuf", [128, 144], H16),
 }
 for _c in range(NCH):
-    for _n, _w, _t in (("abl", 192, H16), ("oab", 128, U16), ("oen", 128, U16), ("ot", 64, U16), ("ou", 64, U16),
-                       ("xa", 1040, B16), ("d", 1024, B16), ("ld", 1024, H16), ("ga", 1024, B16), ("gb", 1024, B16),
-                       ("Ls", 1024, B16), ("lg", 1024, H16), ("en", 2048, H16), ("t", 1024, H16),
-                       ("PA", 2048, F32), ("PB", 2048, F32), ("xu", 1040, B16), ("lp", 1040, H16), ("ad", 1024, H16),
-                       ("sh", 1280, H16), ("sf", 1280, F32), ("si", 448, I32), ("bd", 512, H16), ("pay", 256, F32),
-                       ("nw", 192, H16), ("res", 192, F32), ("eb", 256, H16), ("oe", 16, U16), ("ee", 256, H16)):
+    for _n, _w, _t in (("abl", 192, H16), ("cn", 256, H16), ("ol", 192, U16), ("ot", 64, U16), ("ou", 128, U16),
+                       ("Pa", 1024, F32), ("Pd", 1024, F32), ("d", 1024, I32), ("Rc", 1040, H16), ("gs", 1024, H16),
+                       ("en", 2048, H16), ("t", 1024, H16), ("PP", 4096, F32),
+                       ("xw", 1024, B16), ("dl", 1040, B16), ("ad", 1024, H16),
+                       ("sh", 1536, H16), ("sf", 640, F32), ("si", 512, I32), ("bd", 512, H16), ("pay", 256, F32),
+                       ("res", 192, F32), ("eb", 320, H16), ("oe", 16, U16), ("ee", 256, H16)):
         SCRATCH["%s%d" % (_n, _c)] = ("sbuf", [128, _w], _t)
     SCRATCH["so%d" % _c] = ("sbuf", [128, 192, 16], F32)
+    SCRATCH["tq%d" % _c] = ("sbuf", [128, 32, 16], F32)
     for _r in range(RO):
         SCRATCH["R%d%d" % (_c, _r)] = ("sbuf", [128, 1280], F32)
         SCRATCH["S%d%d" % (_c, _r)] = ("sbuf", [128, 192], F32)
@@ -57,10 +58,12 @@ def ap(name, c0, c1, st=1, p0=0, p1=128):
 
 
 def ap3(name, r0, r1, rs, k0, k1):
+    inner = SCRATCH[name][1][2]
     m = 0
     for r in range(r0, r1, rs):
-        m |= ((1 << (k1 - k0)) - 1) << (16 * r + k0)
-    idx = (slice(0, 128), slice(r0, r1, rs), k0 if k1 - k0 == 1 else slice(k0, k1))
+        m |= ((1 << (k1 - k0)) - 1) << (inner * r + k0)
+    rows = r0 if len(range(r0, r1, rs)) == 1 else slice(r0, r1, rs)
+    idx = (slice(0, 128), rows, k0 if k1 - k0 == 1 else slice(k0, k1))
     return {"n": name, "i": idx, "p": (0, 128), "m": m, "w": len(range(r0, r1, rs)) * (k1 - k0)}
 
 
@@ -69,12 +72,13 @@ def ind(win, off):
 
 
 def two(a):
-    return a["n"][:3] != "ps:" and SCRATCH[a["n"]][2] in (H16, B16, U16)
+    return "n" in a and a["n"][:3] != "ps:" and SCRATCH[a["n"]][2] in (H16, B16, U16)
 
 
 def build(opt):
     ops = []
     cy = 0.83
+    cur = [-1]
 
     def add(eng, ins, cost, **kw):
         rd, wr = [], []
@@ -83,49 +87,52 @@ def build(opt):
             wr.append(aps[0])
             for x in aps[1:]:
                 rd.extend([x["win"], x["off"]] if "win" in x else [x])
-        op = {"e": eng, "ins": ins, "c": cost, "rd": rd, "wr": wr, "id": len(ops), "ch": kw.get("ch", -1)}
+        op = {"e": eng, "ins": ins, "c": cost, "rd": rd, "wr": wr, "id": len(ops), "ch": cur[0]}
         op.update(kw)
         ops.append(op)
         return op
 
-    cur = [-1]
-
     def vcost(out, x, n2):
         if "win" in x:
-            return 50 + x["w"] * max(opt["gam"], opt["ttg"]) * cy
+            return 50 + x["w"] * opt["gam"] * cy
         return max(64, x["w"] * n2) * cy
 
     def tt(out, x, y, o):
         ps = "win" not in x and (x["n"][:3] == "ps:" or y["n"][:3] == "ps:")
-        add("V", [("tt", (out, x, y, o))], vcost(out, x, 1 if ps else 2), ch=cur[0])
+        add("V", [("tt", (out, x, y, o))], vcost(out, x, 1 if ps else 2))
 
     def ts(out, x, s1, o1, s2=None, o2=None):
-        add("V", [("ts", (out, x, s1, s2, o1, o2))], vcost(out, x, 0.5 if two(out) and two(x) else 1), ch=cur[0])
+        add("V", [("ts", (out, x, s1, s2, o1, o2))], vcost(out, x, 0.5 if two(out) and two(x) else 1))
 
     def cp(out, x):
-        add("V", [("cp", (out, x))], vcost(out, x, 0.5 if two(out) and two(x) else 1), ch=cur[0])
+        add("V", [("cp", (out, x))], vcost(out, x, 0.5 if two(out) and two(x) else 1))
 
     def ms(out, v):
-        add("V", [("ms", (out, v))], vcost(out, out, 0.5 if two(out) else 1), ch=cur[0])
+        add("V", [("ms", (out, v))], vcost(out, out, 0.5 if two(out) else 1))
 
     def act(out, x, f=F.Copy, scale=1.0, bias=0.0):
         c = 65 + x["w"] * opt["gam"] * cy if "win" in x else max(64, x["w"]) * cy
-        add("S", [("act", (out, x, f, bias, scale))], c, ch=cur[0])
+        add("S", [("act", (out, x, f, bias, scale))], c)
 
     def lin(out, x, scale, bias):
-        if opt["act_small"]:
-            act(out, x, F.Identity if bias else F.Copy, scale, bias)
-        else:
-            ts(out, x, scale, A.mult, bias, A.add)
+        act(out, x, F.Identity if bias else F.Copy, scale, bias)
 
-    def mm(lst):
+    def offs(out, x):
+        if opt["u16"] == "S":
+            act(out, x)
+        else:
+            cp(out, x)
+
+    def mm(lst, after=None):
         c = 0
         for out, l, r, s, e in lst:
             c += max(min(64, l["w"]), r["w"]) * (1 if two(r) else 4) * opt["pe"]
-        add("P", [("mm", x) for x in lst], c, ch=cur[0])
+        op = add("P", [("mm", x) for x in lst], c)
+        if after:
+            op["after"] = after
 
-    def grp(out, terms):
-        return [(out, l, r, i == 0, i == len(terms) - 1) for i, (l, r) in enumerate(terms)]
+    def grp(out, terms, first=True, last=True):
+        return [(out, l, r, first and i == 0, last and i == len(terms) - 1) for i, (l, r) in enumerate(terms)]
 
     def sel(out, x, pat, o, base, cm):
         add("Q", [("sel", (out, x, pat, o, 0.0, base, cm))], 170 + 2 * cy * out["w"])
@@ -133,18 +140,24 @@ def build(opt):
     def iota(out, pat, base, cm):
         add("Q", [("iota", (out, pat, base, cm))], 130 + 2 * cy * out["w"])
 
+    def conv(e, out, x):
+        if e == "S":
+            act(out, x)
+        else:
+            sel(out, x, [[0, out["w"]]], A.is_ge, 0, 0)
+
     def dma(q, sem, out, src, lat):
         o = {"n": "hbm", "p": (0, 0), "m": 0, "w": 0}
         add(q, [("dma", (out if isinstance(out, dict) else o, src if isinstance(src, dict) else o, (out, src)))], 60,
-            sem=sem, lat=lat, ch=cur[0])
+            sem=sem, lat=lat)
 
-    dma("Y", "la", ap("lin", 0, 128), ("pa",), 2200)
-    dma("Y", "lx", ap("X", 0, W), ("xrec",), 3200)
-    dma("Y", "lb", ap("lin", 128, 256), ("pb",), 2300)
-    dma("Y", "ll", ap("lin", 256, 384), ("lam",), 2400)
-    dma("Y", "le", ap("e96", 0, 96), ("erec",), 2500)
-    dma("Y", "ln", ap("EN", W, 2 * W), ("nbr",), 5500)
-    dma("Y", "lg", ap("G", 0, W), ("grec",), 6000)
+    for sem, o, n, lat in (("le", ap("e96", 0, 96), "erec", 2300), ("lx", ap("X", 0, W), "xrec", 3600),
+                           ("lg", ap("G", 0, W), "grec", 4600), ("ln", ap("EN", W, 2 * W), "nbr", 6600)):
+        dma("Y", sem, o, (n,), lat)
+        if sem != "le":
+            ops[-1]["lag"] = [ops[-2]["id"]]
+    for q, (sem, n) in enumerate((("la", "pa"), ("lb", "pb"), ("ll", "lam"))):
+        dma("S", sem, ap3("lin", 0, 2, 1, 64 * q, 64 * q + 64), (n,), 2800)
     ms(ap("EN", 0, W), 0)
     ts(ap("ehl", 0, 96), ap("e96", 0, 96), 10, A.logical_shift_right)
     ts(ap("ehl", 96, 192), ap("e96", 0, 96), 1023, A.bitwise_and)
@@ -165,74 +178,90 @@ def build(opt):
     ts(ap("pi", 4, 5), ap("pi", 0, 1), 15, A.bitwise_and)
     cp(ap("col", 0, 1), ap("pi", 4, 5))
     ts(ap("MK", 0, 16), ap("MK", 16, 32), ap("col", 0, 1), A.is_equal)
-    for i, v in enumerate((1.0, 8.0, -1.0, 7.0, -7.0)):
-        ts(ap("ID", 128 * i, 128 * i + 128), IF, v, A.mult)
-    I1, I8, IN, I7, IN7 = [ap("ID", 128 * i, 128 * i + 128) for i in range(5)]
-    cp(ap("BOh", 0, 128), BO)
+    I1, IG, IN, IM8, IK, IM2 = [ap("ID", 128 * i, 128 * i + 128) for i in range(6)]
+    act(I1, IF)
+    for o, v in ((IG, 2.0 ** -12), (IN, -1.0), (IM8, -8.0), (IK, float(W)), (IM2, -2.0)):
+        ts(o, I1, v, A.mult)
+    for j in range(3):
+        o, p = 512 * j, ap("ps:pk%d" % j, 0, 512)
+        mm([(p, I1, ap("X", o, o + 512), True, False)])
+        mm([(p, IG, ap("G", o, o + 512), False, True)])
+        if j == 1:
+            ts(ap("PK", o, o + 512), p, 8.0, A.mult, 1028.0, A.add)
+        else:
+            lin(ap("PK", o, o + 512), p, 8.0, 1028.0)
+    lin(ap("BOh", 0, 128), BO, 0.125, 0.0)
     for k in range(16):
         ts(ap("BC", 128 * k, 128 * k + 128), ap("BOh", 0, 128), ap("MK", k, k + 1), A.mult)
         act(ap("DG", 128 * k, 128 * k + 128), IF, F.Copy, ap("MK", k, k + 1))
-    ts(ap("col", 1, 2), ap("MK", 0, 1), 1024.0, A.mult, ap("MK", 1, 2), A.add)
-    ts(ap("col", 2, 3), ap("MK", 15, 16), -1.0, A.mult, 1.0, A.add)
-    ts(ap("col", 3, 4), ap("MK", 0, 1), ap("MK", 15, 16), A.add)
+    m0c, m15 = ap("MK", 0, 1), ap("MK", 15, 16)
+    ts(ap("col", 1, 2), m0c, 1024.0, A.mult, ap("MK", 1, 2), A.add)
+    ts(ap("col", 2, 3), m15, -1.0, A.mult, 1.0, A.add)
+    ts(ap("col", 3, 4), m0c, m15, A.add)
+    ts(ap("col", 4, 5), ap("col", 0, 1), 2.0, A.add)
+    n15 = ap("col", 2, 3)
     ms(ap("UH", 0, 144), 0.0)
-    ms(ap("UE", 0, 144), 0.0)
-    ms(ap("ONE", 0, 64), 1.0)
-    ts(ap("UH", 15, 128, 16), ap("BO", 0, 128, 16), 1.0 / 128, A.mult)
-    ts(ap("UE", 15, 128, 16), ap("BO", 0, 128, 16), ap("col", 1, 2), A.mult)
+    ms(ap("UE", 0, 432), 0.0)
     ms(ap("VE", 0, 144), 0.0)
-    ts(ap("VE", 15, 128, 16), ap("BO", 0, 128, 16), ap("MK", 0, 1), A.mult)
-    ts(ap("VE", 17, 130, 16), ap("BO", 0, 128, 16), ap("MK", 15, 16), A.mult)
-    cp(ap("BO8", 0, 8), ap("BO", 0, 128, 16))
-    tt(ap("PMI", 0, 64), ap("IF", 64, 128), ap("IF", 0, 64), A.subtract)
-    for i, v in enumerate((1.0, -1.0, 8.0, -7.0)):
-        ts(ap("MD", 128 * i, 128 * i + 128), IF, ap("col", 3, 4), A.mult, v, A.mult)
-    ts(ap("MD", 512, 640), IF, -0.5, A.mult)
-    ts(ap("ID", 640, 768), IF, 1536.0, A.mult)
-    ts(ap("ID", 768, 896), IF, -8.0, A.mult)
+    ms(ap("ONE", 0, 64), 1.0)
+    ms(ap("ONE", 64, 128), 2048.0)
+    B8 = ap("BO", 0, 128, 16)
+    ts(ap("UH", 15, 128, 16), B8, 1.0 / 128, A.mult)
+    for i, v in enumerate((1.0, -1.0, 8.0)):
+        ts(ap("UE", 144 * i + 15, 144 * i + 128, 16), B8, ap("col", 1, 2), A.mult, v, A.mult)
+    ts(ap("VE", 15, 128, 16), B8, m0c, A.mult)
+    ts(ap("VE", 17, 130, 16), B8, m15, A.mult)
+    act(ap("BO8", 0, 8), B8)
+    lin(ap("PMI", 0, 128), IF, -1.0, 0.0)
+    M1, MN = ap("MD", 0, 128), ap("MD", 128, 256)
+    ts(M1, I1, ap("col", 3, 4), A.mult)
+    ts(MN, IN, ap("col", 3, 4), A.mult)
     sel(ap("SH", 384, 512), BO, [[-1, 128]], A.is_equal, -1, 1)
     sel(ap("SH", 0, 128), BO, [[-1, 128]], A.is_equal, 1, 1)
     sel(ap("SH", 128, 256), BO, [[-1, 128]], A.is_equal, -15, 1)
     sel(ap("SH", 256, 384), BO, [[-1, 128]], A.is_equal, 15, 1)
     sel(ap("LT", 0, 128), BO, [[1, 128]], A.is_gt, 0, -1)
     tt(ap("SH", 0, 128), ap("SH", 384, 512), ap("SH", 0, 128), A.subtract)
-    ts(ap("SH", 128, 256), ap("SH", 128, 256), -1.0, A.mult)
-    iota(ap("NB", 128, 192), [[16, 64]], 63, 0)
-    iota(ap("NB", 192, 256), [[15, 64]], 63, 0)
-    ts(ap("NB", 0, 64), ap("NB", 192, 256), ap("MK", 0, 1), A.mult)
-    tt(ap("NB", 0, 64), ap("NB", 128, 192), ap("NB", 0, 64), A.subtract)
-    ts(ap("NBh", 0, 64), ap("NB", 0, 64), ap("col", 0, 1), A.add)
-    ts(ap("NB", 64, 128), ap("NB", 192, 256), ap("MK", 0, 1), A.mult, 2.0, A.add)
-    ts(ap("NB", 128, 192), ap("NB", 192, 256), -1.0, A.mult, 1071.0, A.add)
-    ts(ap("NB", 128, 192), ap("NB", 128, 192), ap("MK", 15, 16), A.mult)
-    tt(ap("NB", 64, 128), ap("NB", 64, 128), ap("NB", 128, 192), A.add)
-    EQ, EQ1, L4, M4, IR, WK, WK2 = [ap("q4", 64 * i, 64 * i + 64) for i in range(7)]
-    n15, m15 = ap("col", 2, 3), ap("MK", 15, 16)
+    lin(ap("SH", 0, 128), ap("SH", 0, 128), 4096.0, 0.0)
+    lin(ap("SH", 128, 256), ap("SH", 128, 256), -4096.0, 0.0)
+    lin(ap("SH", 256, 384), ap("SH", 256, 384), 4096.0, 0.0)
+    PRV, NXT, NA, NBB, NW = [ap("NB", 64 * i, 64 * i + 64) for i in range(5)]
+    iota(NA, [[16, 64]], 63, 0)
+    iota(NBB, [[15, 64]], 63, 0)
+    ts(NW, NBB, m0c, A.mult, ap("col", 0, 1), A.subtract)
+    tt(PRV, NA, NW, A.subtract)
+    lin(NBB, NBB, -1.0, 1071.0)
+    ts(NW, NBB, m15, A.mult, ap("col", 4, 5), A.add)
+    tt(NXT, NA, NW, A.add)
+    EQ, EQ1, L4, M4, IR, WK, WQ = [ap("q4", 64 * i, 64 * i + 64) for i in range(7)]
     tt(EQ, ap("IF", 0, 64), ap("IF", 64, 128), A.add)
     tt(EQ1, ap("SH", 384, 448), ap("SH", 448, 512), A.add)
     tt(L4, ap("LT", 0, 64), ap("LT", 64, 128), A.add)
     tt(M4, ap("BO", 0, 64), ap("BO", 64, 128), A.add)
     iota(IR, [[0, 4], [1, 16]], 0, 0)
     tt(IR, IR, M4, A.mult)
-    ts(ap("WC", 0, 64), EQ, 2.0 ** -18, A.mult)
-    ts(ap("WC", 64, 128), EQ1, 2.0 ** -18, A.mult)
-    ts(ap("WH", 0, 64), EQ, 2.0 ** -26, A.mult)
-    ts(ap("WH", 64, 128), L4, 2.0 ** -19, A.mult)
-    ts(ap("WL", 128, 192), L4, 2.0 ** -19, A.mult)
-    ts(ap("WH", 128, 192), IR, 128.0, A.mult, n15, A.mult)
+    lin(ap("WC", 0, 64), EQ, 2.0 ** -18, 0.0)
+    lin(ap("WC", 64, 128), EQ1, 2.0 ** -26, 0.0)
+    lin(ap("WH", 0, 64), EQ, 2.0 ** -15, 0.0)
+    lin(WQ, L4, 2.0, 0.0)
+    tt(WQ, WQ, EQ, A.add)
+    lin(ap("WH", 64, 128), WQ, 15 * 2.0 ** -19, 0.0)
+    lin(ap("WL", 128, 192), WQ, 15 * 2.0 ** -19, 0.0)
+    ts(ap("WH", 128, 192), IR, 2.0 ** -18, A.mult, n15, A.mult)
     ms(ap("WH", 143, 192, 16), 0.0)
-    cp(ap("WL", 192, 256), ap("WH", 128, 192))
+    act(ap("WL", 192, 256), ap("WH", 128, 192))
     ts(ap("WL", 64, 128), IR, 0.125, A.mult, m15, A.mult)
     ts(WK, EQ, 2.0 ** -19, A.mult, n15, A.mult)
     tt(ap("WL", 0, 64), WK, ap("WL", 64, 128), A.add)
-    ts(WK, M4, 4.0, A.mult, m15, A.mult)
-    ts(WK2, L4, -1920.0, A.mult)
-    tt(WK, WK, WK2, A.add)
-    ts(WK2, M4, 128.0, A.mult, n15, A.mult)
+    wz0, wz1 = ap("ps:wz", 0, 64), ap("ps:wz", 64, 128)
+    ts(wz0, M4, 4.0, A.mult, m15, A.mult)
+    lin(WK, L4, -1920.0, 0.0)
+    tt(WK, WK, wz0, A.add)
+    ts(wz1, M4, 128.0, A.mult, n15, A.mult)
     for k in range(14):
-        tt(ap("WZ", 64 * k, 64 * k + 64), WK if k == 0 else ap("WZ", 64 * k - 64, 64 * k), WK2, A.add)
+        tt(ap("WZ", 64 * k, 64 * k + 64), WK if k == 0 else ap("WZ", 64 * k - 64, 64 * k), wz1, A.add)
 
-    Xw, Gw = ap("X", 0, W), ap("G", 0, W)
+    Xw, Pw = ap("X", 0, W), ap("PK", 0, W)
     for c in range(NCH):
         cur[0] = c
         s = str(c)
@@ -240,214 +269,217 @@ def build(opt):
         def a_(n, c0, c1, st=1, p0=0, p1=128):
             return ap(n + s, c0, c1, st, p0, p1)
 
-        def sh(i, n=1):
-            return a_("sh", 64 * i, 64 * (i + n))
+        def sh(i, n=1, p0=0, p1=128):
+            return a_("sh", 64 * i, 64 * (i + n), 1, p0, p1)
 
         def sf(i, n=1):
             return a_("sf", 64 * i, 64 * (i + n))
 
         def si(i, n=1):
             return a_("si", 64 * i, 64 * (i + n))
-        av, bv, lv = a_("abl", 0, 64), a_("abl", 64, 128), a_("abl", 128, 192)
-        for n in ("xa", "xu", "lp"):
-            ms(a_(n, 1024, 1040), 0.0)
+
+        def eb(i, n=1):
+            return a_("eb", 64 * i, 64 * (i + n))
+        ra, rb, rl = a_("abl", 0, 64), a_("abl", 64, 128), a_("abl", 128, 192)
+        av, bv, lv, l8 = [a_("cn", 64 * i, 64 * i + 64) for i in range(4)]
         ms(a_("bd", 0, 512), 0.0)
+        ms(ap3("tq" + s, 0, 32, 1, 0, 16), 0.0)
         for k in (0, 15):
-            ms(ap3("so" + s, 14, 192, 16, k, k + 1), 0.0)
-            ms(ap3("so" + s, 78, 128, 16, k, k + 1), 2.0 ** -26)
-        for q in range(2):
-            cp(a_("oab", 64 * q, 64 * q + 64), ap("lin", 128 * q + 64 * c, 128 * q + 64 * c + 64))
-        for q in range(3):
-            cp(a_("abl", 64 * q, 64 * q + 64), ap("lin", 128 * q + 64 * c, 128 * q + 64 * c + 64))
+            ms(ap3("so" + s, 14, 64, 16, k, k + 1), 0.0)
+            ms(ap3("so" + s, 78, 128, 16, k, k + 1), 2.0 ** -15)
+            ms(ap3("so" + s, 142, 192, 16, k, k + 1), 1920 * 2.0 ** -26)
+        act(a_("abl", 0, 192), ap3("lin", c, c + 1, 1, 0, 192))
+        st2 = "su" if opt["st2"] else "st"
+        mm(grp(ap("ps:%s%s0" % (st2, s), 192, 256), [(I1, rb), (IN, ra)]))
         for r in range(RO):
-            u = s + str(r)
+            u, un = s + str(r), s + str(r + 1)
 
             def ps(n, c0, c1, st=1, p0=0, p1=128):
                 return ap("ps:" + n + u, c0, c1, st, p0, p1)
+
+            def cn(i, n=1, p0=0, p1=128):
+                return ps("cn", 64 * i, 64 * (i + n), 1, p0, p1)
+
+            def send(v):
+                add("Q", [("xfer", (ap("R" + v, 0, 128), ap("S" + v, 0, 192), v)), ("none", (ap("R" + v, 1152, 1280),))],
+                    1000, sem="h" + v, lat=opt["lat"])
             Rw, Sd = "R" + u, "S" + u
-            m8, m0, sg, dif, md8, md0, l8 = sh(0), sh(1), sh(2), sh(3), sh(4), sh(5), sh(6)
+            m8, pas = sh(18 + r), sh(21 + r)
+            m0, md8, md0, zz, sp, sn, spd, sq2, sq1, pd, cm = [sh(i) for i in (0, 1, 2, 3, 4, 5, 6, 7, 11, 12, 13)]
+            lsrc = rl if r == 0 else ps(st2, 128, 192)
+            if opt["st2"]:
+                ts(m8, lsrc, 7.5, A.is_ge)
+                ts(m0, lsrc, 0.5, A.is_lt)
+            else:
+                act(m8, lsrc, F.Relu, 1.0, -7.0)
+                act(m0, lsrc, F.Relu, -1.0, 1.0)
+            if r:
+                act(a_("abl", 0, 192), ps("st", 0, 192))
+            tt(md8, m8, ps(st2, 192, 256), A.mult)
+            tt(md0, m0, ps(st2, 192, 256), A.mult)
+            mm(grp(cn(1), [(I1, ra), (I1, md8)]) + grp(cn(2), [(I1, rb), (IN, md8)]) +
+               grp(cn(0), [(I1, rb), (IK, m8), (IK, m0), (IN, md0)]) + grp(cn(3), [(I1, rl), (IM8, m8)]))
+            offs(a_("ol", 0, 192), cn(0, 3))
+            act(a_("cn", 0, 192), cn(1, 3))
+            mm(grp(cn(4), [(I1, bv), (IN, av), (I1, md8), (IN, md0)]) + grp(cn(5), [(I1, bv), (IN, av)]))
+            on, oa, ob = 0, 64, 128
             for h in range(2):
                 o = 512 * h
-                act(a_("xa", o, o + 512), ind(Xw, a_("oab", 32 * h, 32 * h + 32)))
-                if h < opt["d_act"]:
-                    act(a_("ad", o, o + 512), ind(Xw, a_("oab", 64 + 32 * h, 96 + 32 * h)))
-                    mm(grp(ps("dd%d" % h, 0, 512), [(I1, a_("ad", o, o + 512)), (IN, a_("xa", o, o + 512))]))
-                    act(a_("d", o, o + 512), ps("dd%d" % h, 0, 512))
-                else:
-                    tt(a_("d", o, o + 512), ind(Xw, a_("oab", 64 + 32 * h, 96 + 32 * h)), a_("xa", o, o + 512), A.subtract)
+                (act if opt["pa"][h] == "S" else cp)(a_("Pa", o, o + 512), ind(Pw, a_("ol", oa + 32 * h, oa + 32 * h + 32)))
+                tt(a_("Pd", o, o + 512), ind(Pw, a_("ol", ob + 32 * h, ob + 32 * h + 32)), a_("Pa", o, o + 512), A.subtract)
+            late = r == 0
             for h in range(2):
+                lb_, vs = ps("L%d" % h, 0, 512), ap(Rw, 128 + h, 1152, 2)
                 mm([(ps("L%d" % h, j, 512, 8), ap("BC", 128 * (2 * j + h), 128 * (2 * j + h) + 128), lv, True, True)
                     for j in range(8)])
-                if opt["dg_act"] and opt["ls_first"]:
-                    act(a_("Ls", h, 1024, 2), ps("L%d" % h, 0, 512))
-                tt(a_("ld", h, 1024, 2), a_("d", h, 1024, 2), ps("L%d" % h, 0, 512), A.mult)
-                if opt["dg_act"] and not opt["ls_first"]:
-                    act(a_("Ls", h, 1024, 2), ps("L%d" % h, 0, 512))
-            late = r == 0 or not opt["early"]
-            for h in range(2):
-                mm([(ps("R%d" % h, 0, 512), I8, a_("xa", h, 1024, 2), True, False),
-                    (ps("R%d" % h, 0, 512), I1, a_("ld", h, 1024, 2), False, not (opt["t_act"] and opt["racc"]))])
                 if late:
-                    act(ap(Sd, 128 * h, 128 * h + 64), ps("R%d" % h, 7 * h, 512, 8))
-                act(ap(Rw, 128 + h, 1152, 2), ps("R%d" % h, 0, 512))
-                if not opt["t_act"]:
-                    act(a_("ad", h, 1024, 2), ps("R%d" % h, 0, 512))
-            act(m8, lv, F.Relu, 1.0, -7.0)
-            act(m0, lv, F.Relu, -1.0, 1.0)
-            act(sh(8), lv, F.Relu, 8.0, -56.0)
-            tt(sh(7), lv, sh(8), A.subtract)
-            lin(l8, sh(7), -1.0, 8.0)
-            tt(dif, bv, av, A.subtract)
-            tt(md8, m8, dif, A.mult)
-            tt(md0, m0, dif, A.mult)
-            IK = ap("ID", 640, 768)
-            mm(grp(ps("ls", 0, 64), [(I1, av), (I1, md8)]) + grp(ps("ls", 64, 128), [(I1, bv), (IK, m8), (IK, m0), (IN, md0)]))
-            cp(a_("oen", 0, 128), ps("ls", 0, 128))
-            for q in range(2):
-                act(a_("en", 1024 * q, 1024 * q + 1024), ind(ap("EN", 0, 2 * W), a_("oen", 64 * q, 64 * q + 64)))
+                    e = ap(Sd, 128 * h, 128 * h + 64)
+                    tt(e, a_("Pd", 15 * h, 1024, 16), ps("L%d" % h, 7 * h, 512, 8), A.mult)
+                    tt(e, e, a_("Pa", 15 * h, 1024, 16), A.add)
+                tt(lb_, a_("Pd", h, 1024, 2), lb_, A.mult)
+                tt(vs, a_("Pa", h, 1024, 2), lb_, A.add)
+                conv(opt["rc"][h], a_("Rc", h, 1024, 2), vs)
+
+            def half(n, h, o=0):
+                return ap(n, o + 512 * h, o + 512 * h + 512)
+
+            def prod(q, h):
+                return half("PP" + s, h, 1024 * q)
+
+            def total(q):
+                mm([(ps("s%d" % q, j, 64, 8), a_("PP", 1024 * q + j, 1024 * q + 1024, 8), ap("BO8", 0, 8), True, True)
+                    for j in range(8)])
+                if q % 2 == 0:
+                    act(sf(4 + q // 2), ps("s%d" % q, 0, 64))
+                    return
+                for j in range(2):
+                    o = 8 * (q - 1 + j)
+                    tt(ap3("tq" + s, o, o + 8, 1, 8 * j, 8 * j + 8), sf(4 + q // 2), ps("s%d" % q, 0, 64), A.mult)
+                mm(grp(ps("df", 0, 64), [(ap3("tq" + s, 8 * (q - 1 + j), 8 * (q + j), 1, 0, 16),
+                                          ap("PMI", j, 128, 2) if q == 1 else ap("IF", j, 128, 2)) for j in range(2)], q == 1, q == 3))
+            for h in range(2):
+                gb = ps("g%d" % h, 0, 512)
+                conv(opt["d"][h], half("d" + s, h), half("Pd" + s, h))
+                if opt["g"][h] == "P":
+                    mm([(gb, IF, half(Rw, h, 128), True, False)])
+                    mm([(gb, IN, half("Rc" + s, h), False, True)])
+                    act(half("gs" + s, h), gb)
+                else:
+                    mm([(ps("r%d" % h, 0, 512), I1, half("Rc" + s, h), True, True)])
+                    tt(half("gs" + s, h), half(Rw, h, 128), ps("r%d" % h, 0, 512), A.subtract)
+                    mm([(gb, I1, half("gs" + s, h), True, True)], half("d" + s, h))
+                tt(prod(0, h), half("d" + s, h), gb, A.mult)
+            total(0)
+            lin(l8, lv, -1.0, 8.0)
+            act(zz, lv, F.Relu, -1.0, 1.0)
+            for h in range(2):
+                (act if opt["en"][h] == "S" else cp)(a_("en", 512 * h, 512 * h + 512),
+                                                     ind(ap("EN", 0, W), a_("ol", oa + 32 * h, oa + 32 * h + 32)))
+            act(a_("en", 1024, 2048), ind(ap("EN", 0, 2 * W), a_("ol", on, on + 64)))
             for q in range(2):
                 mm(grp(ps("E", 64 * q, 64 * q + 64),
                        [(ap("UE", 15 - k, 143 - k), a_("en", 1024 * q + k, 1024 * q + 1024, 16)) for k in range(16)]))
-            tt(sf(0, 2), ps("E", 0, 128), sh(6, 2), A.mult)
-            def send(v):
-                add("Q", [("xfer", (ap("R" + v, 0, 128), ap("S" + v, 0, 192), v)), ("none", (ap("R" + v, 1152, 1280),))],
-                    1000, sem="h" + v, lat=opt["lat"], ch=c)
+                tt(sf(q), ps("E", 64 * q, 64 * q + 64), (l8, lv)[q], A.mult)
             if late:
                 tt(ap(Sd, 64, 128), sf(0), sf(1), A.add)
                 send(u)
-                et = [(ap("SH", 0, 128), ap(Sd, 64, 128))]
-            else:
-                et = [(ap("SH", 0, 128), sf(0)), (ap("SH", 0, 128), sf(1))]
-            mm(grp(ps("N", 0, 64),
-                   [(ap("DG", 128 * k, 128 * k + 128), a_("en", 1024 + k, 2048, 16)) for k in range(16)]))
-            nma, sg = sh(11), si(0)
-            tt(nma, ps("N", 0, 64), av, A.subtract)
-            ts(sg, lv, 1.0 / 7, A.mult, -4.0 / 7, A.add)
+            mm(grp(cn(6), [(ap("DG", 128 * k, 128 * k + 128), a_("en", 1024 + k, 2048, 16)) for k in range(16)] + [(IN, av)]))
+            tt(cn(6), zz, cn(6), A.mult)
             for h in range(2):
                 o = 64 * h
-                act(a_("bd", 384 + o, 448 + o, 1, o, o + 64), a_("abl", 0, 64, 1, o, o + 64))
-            act(a_("ga", 0, 1024), ind(Gw, a_("oab", 0, 64)))
-            if opt["dg_act"]:
-                act(a_("gb", 0, 1024), ind(Gw, a_("oab", 64, 128)))
-                for h in range(2):
-                    mm(grp(ps("dg%d" % h, 0, 512), [(I1, a_("gb", h, 1024, 2)), (IN, a_("ga", h, 1024, 2))]))
-                    tt(a_("lg", h, 1024, 2), a_("Ls", h, 1024, 2), ps("dg%d" % h, 0, 512), A.mult)
-            else:
-                tt(a_("gb", 0, 1024), ind(Gw, a_("oab", 64, 128)), a_("ga", 0, 1024), A.subtract)
-                for h in range(2):
-                    tt(a_("lg", h, 1024, 2), a_("gb", h, 1024, 2), ps("L%d" % h, 0, 512), A.mult)
-            mm(grp(ps("ed", 0, 64), et + [(ap("SH", 128, 256), ap(Rw, 0, 64)), (ap("SH", 256, 384), ap(Rw, 1216, 1280))]))
-            ts(sf(2), ps("ed", 0, 64), 0.0, A.is_ge)
-            tt(sh(2), sf(2), ap("NB", 64, 128), A.mult)
-            mm(grp(ps("ed", 64, 128), [(I1, ap("NBh", 0, 64)), (I1, sh(2))]))
-            cp(a_("ot", 0, 64), ps("ed", 64, 128))
+                act(a_("bd", 384 + o, 448 + o, 1, o, o + 64), a_("cn", 0, 64, 1, o, o + 64))
+            ed = ps("ed", 0, 64)
+            halo = [(ap("SH", 128, 256), ap(Rw, 0, 64)), (ap("SH", 256, 384), ap(Rw, 1216, 1280))]
+            own = [(ap("SH", 0, 128), sf(1))]
+            mm(grp(ed, [(I1, ap("ONE", 64, 128)), (ap("SH", 0, 128), sf(0))] + (own if late else halo), True, False))
+            mm(grp(ed, halo if late else own, False, True))
+            tt(ed, ed, PRV, A.max)
+            tt(ed, ed, NXT, A.min)
+            offs(a_("ot", 0, 64), ed)
             for h in range(2):
                 o = 512 * h
-                if opt["t_act"]:
-                    act(a_("t", o, o + 512), ind(ap(Rw, 64, 1216), a_("ot", 32 * h, 32 * h + 32)))
+                act(a_("t", o, o + 512), ind(ap(Rw, 64, 1216), a_("ot", 32 * h, 32 * h + 32)))
+            for h in range(2):
+                tb = ps("t%d" % h, 0, 512)
+                mm(grp(tb, [(I1, half("t" + s, h)), (IN, half("Rc" + s, h))]))
+                tt(prod(2, h), half("gs" + s, h), tb, A.mult)
+                act(prod(1, h), tb, F.Square)
+                tt(prod(3, h), half("d" + s, h), tb, A.mult)
+            for q in (2, 1, 3):
+                total(q)
+            df = ps("df", 0, 64)
+            ts(sp, df, 0.0, A.is_gt)
+            ts(sn, df, 0.0, A.is_lt)
+            tt(sq1, sn, cn(4), A.mult)
+            tt(sh(6, 2), sh(4, 2), cn(5, 2), A.mult)
+            mm(grp(cn(1), [(I1, av), (I1, sq1)]) + grp(cn(0), [(I1, av), (I1, spd), (I1, sq2)]) +
+               grp(cn(7), [(I1, lv), (I1, sp), (IN, sn)]))
+            offs(a_("ou", 0, 128), cn(0, 2))
+            ts(cm, cn(7), 4.5, A.is_gt)
+            for h in range(2):
+                o = 64 * h
+                tt(a_("bd", o, o + 64, 1, o, o + 64), sh(13, 1, o, o + 64), cn(5, 1, o, o + 64), A.mult)
+            bn, ln = eb(0), eb(1)
+            act(pas, cn(7), F.Relu, -1.0, 0.0)
+            act(ln, cn(7), F.Abs)
+            tt(pd, pas, cn(5), A.mult)
+            mm(grp(cn(2), [(I1, bv), (I1, sq2), (IN, pd)]))
+            act(bn, cn(2))
+            nq = opt["nq"]
+            wq, pq = 1024 // nq, 64 // nq
+            for h in range(nq):
+                o = wq * h
+                act(a_("xw", o, o + wq), ind(Xw, a_("ou", 64 + pq * h, 64 + pq * h + pq)))
+                if opt["dl"][h] == "V":
+                    tt(a_("dl", o, o + wq), ind(Xw, a_("ou", pq * h, pq * h + pq)), a_("xw", o, o + wq), A.subtract)
                 else:
-                    tt(a_("t", o, o + 512), ind(ap(Rw, 64, 1216), a_("ot", 32 * h, 32 * h + 32)), a_("ad", o, o + 512),
-                       A.subtract)
-            for h in range(2 if opt["t_act"] else 0):
-                mm(grp(ps("g%d" % h, 0, 512), [(I8, a_("ga", h, 1024, 2)), (I1, a_("lg", h, 1024, 2))]))
-                act(a_("ad", h, 1024, 2), ps("g%d" % h, 0, 512))
-                tt(a_("PA", h, 1024, 2), a_("d", h, 1024, 2), ps("g%d" % h, 0, 512), A.mult)
-                gr = grp(ps("t%d" % h, 0, 512), [(ap("ID", 768, 896), a_("xa", h, 1024, 2)), (IN, a_("ld", h, 1024, 2)),
-                                                 (I1, a_("t", h, 1024, 2))])
-                if opt["racc"]:
-                    tp = ps("R%d" % h, 0, 512)
-                    mm([(tp, IN, a_("t", h, 1024, 2), False, True)])
-                else:
-                    tp = ps("t%d" % h, 0, 512)
-                    mm(gr[:2])
-                    ops[-1]["after"] = a_("ot", 0, 64)
-                    mm(gr[2:])
-                tt(a_("PA", 1024 + h, 2048, 2), a_("ad", h, 1024, 2), tp, A.mult)
-                tt(a_("PB", 1024 + h, 2048, 2), a_("d", h, 1024, 2), tp, A.mult)
-                act(a_("PB", h, 1024, 2), tp, F.Square)
-            for h in range(0 if opt["t_act"] else 2):
-                mm(grp(ps("g%d" % h, 0, 512), [(I8, a_("ga", h, 1024, 2)), (I1, a_("lg", h, 1024, 2))]))
-                ops[-1]["after"] = a_("ot", 0, 64)
-                tt(a_("PA", h, 1024, 2), a_("d", h, 1024, 2), ps("g%d" % h, 0, 512), A.mult)
-                tt(a_("PA", 1024 + h, 2048, 2), a_("t", h, 1024, 2), ps("g%d" % h, 0, 512), A.mult)
-                act(a_("PB", h, 1024, 2), a_("t", h, 1024, 2), F.Square)
-                mm([(ps("d%d" % h, 0, 512), I1, a_("d", h, 1024, 2), True, True)])
-                ops[-1]["after"] = a_("ot", 0, 64)
-                tt(a_("PB", 1024 + h, 2048, 2), a_("t", h, 1024, 2), ps("d%d" % h, 0, 512), A.mult)
-            for h in range(2):
-                for n in ("PB", "PA"):
-                    mm([(ps("s" + n, k, 128, 16), a_(n, k, 2048, 16), ap("BO8", 0, 8), True, True) for k in range(h, 16, 2)])
-            act(sf(4, 2), ps("sPB", 0, 128))
-            tt(sf(4, 2), sf(4, 2), ps("sPA", 0, 128), A.mult)
-            mm([(ps("df", 0, 64), sf(4, 2), ap("PMI", 0, 64), True, True)])
-            pas, dl, l1, uu, lA, lB = sh(13), sh(14), sh(15), sh(16), sh(17), sh(18)
-            pn, pQ, pQ2, psg = [a_("nw", 0, 64), a_("nw", 64, 128), a_("nw", 128, 192), sh(19)]
-            tt(sf(3), ps("df", 0, 64), sg, A.mult)
-            ts(dl, ps("df", 0, 64), -1.0, A.max, 1.0, A.min)
-            ts(pas, sf(3), 0.0, A.max, 1.0, A.min)
-            tt(l1, lv, dl, A.add)
-            tt(pn, pas, nma, A.mult)
-            mm(grp(ps("uu", 0, 64), [(I1, av), (I1, pn)]))
-            cp(a_("ou", 0, 64), ps("uu", 0, 64))
-            ts(lA, l1, 0.0, A.max, -8.0, A.add)
-            act(lB, lA, F.Abs)
-            act(lA, lB, F.Identity, -1.0, 8.0)
-            tt(pQ, pas, dif, A.mult)
-            tt(pQ2, m8, pn, A.mult)
-            tt(sh(12), m8, pQ, A.mult)
-            ts(psg, l1, 0.0, A.max, 8.0, A.min)
-            ts(dl, l1, 4.5, A.is_gt)
-            for h in range(2):
-                tt(a_("bd", 64 * h, 64 * h + 64, 1, 64 * h, 64 * h + 64), a_("sh", 896, 960, 1, 64 * h, 64 * h + 64),
-                   a_("sh", 192, 256, 1, 64 * h, 64 * h + 64), A.mult)
-            act(a_("xu", 0, 1024), ind(Xw, a_("ou", 0, 64)))
-            for h in range(2):
-                mm([(ps("M%d" % h, j, 512, 8), ap("BC", 128 * (2 * j + h), 128 * (2 * j + h) + 128), lA, True, True)
-                    for j in range(8)])
-                tt(a_("lp", h, 1024, 2), a_("d", h, 1024, 2), ps("M%d" % h, 0, 512), A.mult)
-            M1, MN, M8, MN7, MH = [ap("MD", 128 * i, 128 * i + 128) for i in range(5)]
-
-            mm(grp(ps("nd", 0, 64), [(M1, av), (M1, pn), (MN, pQ2), (M1, sh(12))]) +
-               grp(ps("nd", 64, 128), [(M1, bv), (M1, pQ2), (MN, pQ)]) + grp(ps("nd", 128, 192), [(MN7, l1), (M8, psg)]))
-            act(a_("eb", 0, 192), ps("nd", 0, 192))
-            early = opt["early"] and r < RO - 1
-            if early:
-                Sn = "S" + s + str(r + 1)
-                lin(a_("eb", 192, 256), a_("eb", 128, 192), -1.0, 8.0)
-                mm(grp(ps("el", 0, 16), [(ap("VE", 15 - 4 * j - q, 143 - 4 * j - q), a_("eb", 64 * q + 16 * j, 64 * q + 16 * j + 16))
-                                         for j in range(4) for q in range(2)]))
-                cp(a_("oe", 0, 16), ps("el", 0, 16))
+                    (act if opt["dl"][h] == "S" else cp)(a_("dl", o, o + wq), ind(Xw, a_("ou", pq * h, pq * h + pq)))
+            if r < RO - 1:
+                Sn = "S" + un
+                mm(grp(ps("cn", 192, 208), [(ap("VE", 15 - 4 * j, 143 - 4 * j), a_("eb", 16 * j, 16 * j + 16)) for j in range(4)]))
+                offs(a_("oe", 0, 16), ps("cn", 192, 208))
                 act(a_("ee", 0, 256), ind(ap("EN", 0, W), a_("oe", 0, 16)))
-                gr = []
-                for q in range(2):
-                    for j in range(4):
-                        gr += grp(ps("eE", 64 * (1 - q) + 16 * j, 64 * (1 - q) + 16 * j + 16),
-                                  [(ap("UE", 15, 143), a_("ee", 4 * j + q, 256, 16)), (ap("UE", 0, 128), a_("ee", 4 * j + q + 2, 256, 16))])
+                e0, e15 = a_("en", 0, 1024, 16), a_("en", 15, 1024, 16)
+                gr = grp(ps("eE", 64, 128), [(ap("UE", 303, 431), e0), (ap("UE", 288, 416), e15)])
+                for j in range(4):
+                    o = 256 * j
+                    gr += grp(ps("eE", 16 * j, 16 * j + 16),
+                              [(ap("UE", 159, 287), a_("en", o, o + 256, 16)), (ap("UE", 144, 272), a_("en", o + 15, o + 256, 16)),
+                               (ap("UE", 15, 143), a_("ee", 4 * j, 256, 16)), (ap("UE", 0, 128), a_("ee", 4 * j + 2, 256, 16))])
                 mm(gr)
-                tt(sf(10, 2), ps("eE", 0, 128), a_("eb", 128, 256), A.mult)
-                tt(ap(Sn, 64, 128), sf(10), sf(11), A.add)
+                tt(sf(2), ln, ps("eE", 0, 64), A.mult)
+                tt(ap(Sn, 64, 128), sf(2), ps("eE", 64, 128), A.add)
                 gr = []
                 for h in range(2):
-                    gr += grp(ps("eR", 64 * h, 64 * h + 64), [(I7, a_("xa", 15 * h, 1024, 16)), (I1, a_("lp", 15 * h, 1024, 16)),
-                                                              (I1, a_("xu", 15 * h, 1024, 16))])
+                    n = 1 if len(set(opt["dl"][:nq])) == 1 else nq
+                    for j in range(n):
+                        o, e, p = 1024 // n * j + 15 * h, 1024 // n * (j + 1), 128 + 64 * h + 64 // n * j
+                        gr += grp(ps("eE", p, p + 64 // n), [(I1, a_("Rc", o, e, 16)), (I1, a_("dl", o, e, 16))] +
+                                  ([] if opt["dl"][j] == "V" else [(IN, a_("xw", o, e, 16))]))
                 mm(gr)
                 for h in range(2):
-                    act(ap(Sn, 128 * h, 128 * h + 64), ps("eR", 64 * h, 64 * h + 64))
-                send(s + str(r + 1))
-            for h in range(2):
-                gr = grp(ps("D%d" % h, 0, 512),
-                         [(I7, a_("xa", h + 1, 1025, 2)), (IN7, a_("xa", h, 1024, 2)), (I1, a_("lp", h + 1, 1025, 2)),
-                          (IN, a_("lp", h, 1024, 2)), (I1, a_("xu", h + 1, 1025, 2)), (IN, a_("xu", h, 1024, 2))])
-                mm(gr[:2])
-                ops[-1]["after"] = a_("ou", 0, 64)
-                mm(gr[2:4])
-                mm(gr[4:])
-                act(a_("ad", h, 1024, 2), ps("D%d" % h, 0, 512), F.Abs)
-            gr = grp(ps("H", 0, 64), [(ap("UH", 15 - j, 143 - j), a_("ad", j, 1024, 16)) for j in range(0, 15, 2)] +
-                     [(ap("UH", 0, 128), ap("ONE", 0, 64))] +
-                     [(ap("UH", 15 - j, 143 - j), a_("ad", j, 1024, 16)) for j in range(1, 15, 2)])
-            mm(gr[:9])
-            mm(gr[9:])
+                    act(ap(Sn, 128 * h, 128 * h + 64), ps("eE", 128 + 64 * h, 192 + 64 * h))
+                send(un)
+                ea, ebb, el = [(0, av)], [(0, bn)], [(0, ln)]
+            else:
+                mm(grp(cn(3), [(I1, sh(18 + i)) for i in range(2 * RO)]))
+                cp(si(7), cn(3))
+                ts(si(7), si(7), 1, A.bitwise_and)
+                mm(grp(cn(3), [(I1, bn), (IN, av)]) + grp(cn(4), [(IM2, ln)]))
+                tt(eb(2), si(7), cn(3), A.mult)
+                ts(cn(4), cn(4), 8.0, A.add)
+                tt(eb(3), si(7), cn(4), A.mult)
+                ea, ebb, el = [(0, av), (0, eb(2))], [(0, bn), (128, eb(2))], [(0, ln), (0, eb(3))]
+            for h in range(nq):
+                o, e = wq * h, wq * h + wq
+                db, two_ = ps("D%d" % h, 0, wq - 1), opt["dl"][h] != "V"
+                mm(grp(db, [(I1, a_("Rc", o + 1, e)), (IN, a_("Rc", o, e - 1))], True, False), a_("xw", o, e))
+                if two_:
+                    mm(grp(db, [(IN, a_("xw", o + 1, e)), (I1, a_("xw", o, e - 1))], False, False))
+                mm(grp(db, [(I1, a_("dl", o + 1, e)), (IN, a_("dl", o, e - 1))], False, True))
+                act(a_("ad", o, e - 1), db, F.Abs)
+            mm(grp(ps("H", 0, 64), [(ap("UH", 0, 128), ap("ONE", 0, 64))] +
+                   [(ap("UH", 15 - j, 143 - j), a_("ad", j, 1024, 16)) for j in range(15)]))
             for h in range(2):
                 o = 64 * h
                 ts(a_("bd", 128 + o, 192 + o, 1, o, o + 64), ps("H", 0, 64, 1, o, o + 64), MAGIC, A.add, -MAGIC, A.add)
@@ -455,55 +487,186 @@ def build(opt):
                 o = 64 * h
                 tt(a_("bd", 256 + o, 320 + o, 1, o, o + 64), ps("H", 0, 64, 1, o, o + 64),
                    a_("bd", 128 + o, 192 + o, 1, o, o + 64), A.subtract)
-            cb, hb, lb = a_("bd", 0, 128), a_("bd", 128, 256), a_("bd", 256, 384)
-            ab = a_("bd", 384, 512)
-            mm(grp(ps("py", 0, 64), [(cb, ap("WC", 0, 64)), (ab, ap("WC", 0, 64)), (lb, ap("WL", 0, 64))]) +
-               grp(ps("py", 64, 128), [(cb, ap("WC", 64, 128)), (ab, ap("WC", 64, 128)), (lb, ap("WL", 64, 128)),
-                                       (hb, ap("WH", 0, 64))]) +
-               grp(ps("py", 128, 256), [(lb, ap("WL", 128, 256)), (hb, ap("WH", 64, 192))]))
-            act(a_("pay", 0, 256), ps("py", 0, 256))
+            cb, hb, lb, ab = [a_("bd", 128 * i, 128 * i + 128) for i in range(4)]
+            g0 = [(cb, ap("WC", 0, 64)), (ab, ap("WC", 0, 64)), (lb, ap("WL", 0, 64))]
+            rest = (grp(ps("py", 64, 128), [(cb, ap("WC", 64, 128)), (ab, ap("WC", 64, 128)), (lb, ap("WL", 64, 128)),
+                                            (hb, ap("WH", 0, 64))]) +
+                    grp(ps("py", 128, 256), [(lb, ap("WL", 128, 256)), (hb, ap("WH", 64, 192))]))
+            if opt["py2"]:
+                mm(grp(ps("px", 0, 64), g0))
+                act(a_("pay", 0, 64), ps("px", 0, 64))
+                mm(rest)
+                act(a_("pay", 64, 256), ps("py", 64, 256))
+            else:
+                mm(grp(ps("py", 0, 64), g0) + rest)
+                act(a_("pay", 0, 256), ps("py", 0, 256))
             for h in range(2):
                 wz = ap("WZ", 448 * h, 448 * h + 448)
                 mm(grp(ps("Z%d" % h, 0, 448), [(hb, wz), (lb, wz)]))
-                for q in range(3):
+            for q in range(3):
+                for h in range(2):
                     add("V", [("scan", (ap3("so" + s, 64 * q, 64 * q + 64, 1, 1 + 7 * h + j, 2 + 7 * h + j),
                                         ps("Z%d" % h, 64 * j, 64 * j + 64), a_("pay", 64 * q, 64 * q + 64)))
-                              for j in range(7)], 7 * 64 * cy, ch=c)
-            gp, rc, y, x = sf(6), sf(7), sf(8), sf(9)
-            ts(si(0, 2), ap3("so" + s, 14, 128, 16, 0, 16), 2.0 ** 26, A.mult, 64.0, A.add)
-            lin(y, ap3("so" + s, 142, 192, 16, 0, 16), -15.0 * 2.0 ** 26, 0.0)
-            ts(si(4, 2), si(0, 2), 255, A.bitwise_and)
-            ts(si(2, 2), si(0, 2), 8, A.logical_shift_right, 2047, A.bitwise_and)
-            tt(y, y, a_("pay", 192, 256), A.add)
-            lin(gp, si(5), 128.0, -8256.0)
-            tt(gp, gp, si(4), A.add)
-            ts(gp, gp, 15.0, A.mult, 1.0 / 32, A.max)
-            add("V", [("rcp", (rc, gp))], 190 + 6 * 64 * cy, ch=c)
-            lin(y, y, 8.0, 0.25)
+                              for j in range(7)], 7 * 64 * cy)
+            gp, rc, y = sf(6), sf(7), sf(8)
+            for q in range(2):
+                x = ap3("so" + s, 64 * q + 14, 64 * q + 64, 16, 0, 16)
+                if opt["cvt"] == "S" or q:
+                    lin(si(q), x, 2.0 ** 26, 64.0 - 64 * q)
+                else:
+                    ts(si(q), x, 2.0 ** 26, A.mult, 64.0, A.add)
+            ts(si(4), si(0), 255, A.bitwise_and)
+            ts(si(5), si(1), 4, A.logical_shift_right, 127 * 128, A.bitwise_and)
+            tt(gp, si(4), si(5), A.add)
+            ts(gp, gp, -64.0, A.add, 1.0 / 240, A.max)
+            add("V", [("rcp", (rc, gp))], 190 + 6 * 64 * cy)
+            ts(si(2), si(0), 8, A.logical_shift_right, 2047, A.bitwise_and)
+            ts(si(3), si(1), 2047, A.bitwise_and)
             act(sh(8, 2), si(2, 2))
-            tt(x, y, rc, A.mult)
-            ts(sh(13), x, 1023.97, A.add)
-            ts(sh(10), sh(13), -1023.5, A.add)
-            tt(x, sh(10), gp, A.mult)
-            tt(sh(13), x, y, A.is_le)
-            st = []
-            for q, src in ((0, [8]), (1, [9]), (2, [10, 13])):
-                for h in range(2):
-                    o = 64 * h
-                    st += grp(ps("st", 64 * q, 64 * q + 64, 1, o, o + 64),
-                              [(ap("ID", o, o + 64), a_("eb", 64 * q, 64 * q + 64))] +
-                              ([(ap("MD", 512 + o, 576 + o), ap("ONE", 0, 64))] if q == 2 else []) +
-                              [(a_("sh", 64 * x, 64 * x + 64, 1, o, o + 64), ap("ID", o, o + 64, 1, o, o + 64)) for x in src])
-            mm(st[:8])
-            mm(st[8:])
+            tt(y, a_("pay", 192, 256), ap3("so" + s, 142, 192, 16, 0, 16), A.subtract)
+            lin(y, y, 2.0 ** 28 / 15, 1.0 / 60)
+            tt(si(6), y, rc, A.mult)
+            lin(sh(10), si(6), 1.0, 4.0)
+
+            def turn(n, q, edge, terms):
+                gr = []
+                for o in (0, 64):
+                    gr += grp(ap("ps:" + n + un, 64 * q, 64 * q + 64, 1, o, o + 64),
+                              [(ap("MD", m + o, m + o + 64), x) for m, x in edge] +
+                              [(sh(x, 1, o, o + 64), ap("ID", m + o, m + o + 64, 1, o, o + 64)) for x, m in terms])
+                return gr
+            mm(turn("st", 0, ea, [(8, 0)]) + turn("st", 1, ebb, [(9, 0)]))
             if r < RO - 1:
-                cp(a_("oab", 0, 128), ps("st", 0, 128))
-                act(a_("abl", 0, 192), ps("st", 0, 192))
-            else:
-                act(a_("res", 0, 192), ps("st", 0, 192))
+                mm(turn(st2, 3, [(0, bn), (128, av)], [(9, 0), (8, 256)]))
+                if opt["st2"]:
+                    mm(turn(st2, 2, el, [(10, 0)]))
+            mm(turn("st", 2, el, [(10, 0)]))
+            if r == RO - 1:
+                act(a_("res", 0, 128), ap("ps:st" + un, 0, 128))
+                act(a_("res", 128, 192), ap("ps:st" + un, 128, 192))
                 for q, n in enumerate(("ya", "yb", "yl")):
-                    dma("S" if q == 1 else "Y", "o%d%d" % (c, q), (n, 64 * c), a_("res", 64 * q, 64 * q + 64), 2000)
+                    dma("S" if q == 2 else "Y", "o%d%d" % (c, q), (n, 64 * c, 64 * c + 64), a_("res", 64 * q, 64 * q + 64), 2000)
     return ops
+
+
+STEP = 24
+
+
+def network(ops, gap):
+    anc, pre, names = [], [], {}
+    for op in ops:
+        seen, keep = 0, []
+        for d in sorted(op["dep0"], reverse=True):
+            if not seen >> d & 1 or "lat" in ops[d]:
+                keep.append((d, gap(ops[d], op)))
+            seen |= anc[d] | 1 << d
+        anc.append(seen)
+        pre.append(keep)
+    tile = [names.setdefault(min(op["tiles"]), len(names)) if op["tiles"] else -1 for op in ops]
+    return {"anc": anc, "pre": pre, "tile": tile, "eng": ["VSPQY".index(op["e"]) for op in ops],
+            "cost": [op["c"] for op in ops], "tail": [op.get("lat", 0) for op in ops],
+            "uses": [tile.count(t) for t in range(len(names))], "X": gap({"e": "V"}, {"e": "S"})}
+
+
+def fresh(net):
+    n = len(net["pre"])
+    return ([0.0] * n, [-1] * n, [0.0] * 5, [-1] * 5, net["uses"], [-1] * len(net["uses"]), [0.0] * 8, [-1] * 8,
+            list(range(8)), 0.0, -1)
+
+
+def replay(net, perm, marks, k0):
+    pre, eng, cost, tail, tile, X = net["pre"], net["eng"], net["cost"], net["tail"], net["tile"], net["X"]
+    m = marks[k0]
+    end, why, free, lastop, left, bank, bfree, blast, avail = [list(x) for x in m[:9]]
+    top, topi = m[9], m[10]
+    marks = marks[:k0 + 1]
+    for p0 in range(k0 * STEP, len(perm), STEP):
+        if p0 > k0 * STEP:
+            marks.append((end, why, list(free), list(lastop), list(left), list(bank), list(bfree), list(blast),
+                          list(avail), top, topi))
+        for i in perm[p0:p0 + STEP]:
+            e = eng[i]
+            t, w = free[e], lastop[e]
+            for d, g in pre[i]:
+                x = end[d] + g
+                if x > t:
+                    t, w = x, d
+            tl = tile[i]
+            if tl >= 0:
+                b = bank[tl]
+                if b < 0:
+                    if not avail:
+                        return None
+                    b = avail[0]
+                    for y in avail:
+                        if bfree[y] < bfree[b]:
+                            b = y
+                    avail.remove(b)
+                    bank[tl] = b
+                    if bfree[b] > t:
+                        t, w = bfree[b], blast[b]
+                t += cost[i]
+                if t + X > bfree[b]:
+                    bfree[b], blast[b] = t + X, i
+                left[tl] -= 1
+                if not left[tl]:
+                    avail.append(b)
+            else:
+                t += cost[i]
+            end[i] = free[e] = t
+            lastop[e] = i
+            why[i] = w
+            if t + tail[i] > top:
+                top, topi = t + tail[i], i
+    return top, topi, why, end, bank, marks
+
+
+def improve(net, perm, opt):
+    anc, n = net["anc"], opt["tries"]
+    rnd = np.random.RandomState(opt["seed"]).rand(n, 4).tolist()
+    cur = replay(net, perm, [fresh(net)], 0)
+    best = (cur[0], perm)
+    runs = None
+    for it in range(n):
+        if runs is None:
+            i, why, runs, run = cur[1], cur[2], [], []
+            while why[i] >= 0:
+                if anc[i] >> why[i] & 1:
+                    run = []
+                else:
+                    if not run:
+                        run = [i]
+                        runs.append(run)
+                    run.append(why[i])
+                i = why[i]
+            pairs = [(r, j) for r in runs for j in range(len(r) - 1)]
+        if not pairs:
+            break
+        a, b, c, d = rnd[it]
+        r, j = pairs[int(a * len(pairs))]
+        if b < 0.5:
+            v, u = r[j], r[j + 1 if c < 0.5 else j + 1 + int((2 * c - 1) * (len(r) - j - 1))]
+        else:
+            u, v = r[j + 1], r[j if c < 0.5 else int((2 * c - 1) * (j + 1))]
+        if anc[v] >> u & 1:
+            continue
+        pu = perm.index(u)
+        pv = perm.index(v, pu)
+        mid = perm[pu:pv + 1]
+        if b < 0.5:
+            s = anc[v] | 1 << v
+            new = [x for x in mid if s >> x & 1] + [x for x in mid if not s >> x & 1]
+        else:
+            s = [x == u or anc[x] >> u & 1 for x in mid]
+            new = [x for x, y in zip(mid, s) if not y] + [x for x, y in zip(mid, s) if y]
+        new = perm[:pu] + new + perm[pv + 1:]
+        res = replay(net, new, cur[5], pu // STEP)
+        heat = opt["hot"] * (opt["cold"] / opt["hot"]) ** (it / n)
+        if res and res[0] <= cur[0] - heat * math.log(d + 1e-12):
+            cur, perm, runs = res, new, None
+            if res[0] < best[0]:
+                best = (res[0], new)
+    return best[1]
 
 
 def schedule(ops, opt):
@@ -520,7 +683,7 @@ def schedule(ops, opt):
             for (o2, a2, w2) in hist.get(a["n"], ()):
                 if o2 is op:
                     continue
-                if isps and o2["e"] != op["e"]:
+                if isps and (o2["e"] != op["e"] or op["e"] == "P"):
                     dep.add(o2["id"])
                 elif (w or w2) and a["m"] & a2["m"] and a["p"][0] < a2["p"][1] and a2["p"][0] < a["p"][1]:
                     if "nowaw" in a and "nowaw" in a2:
@@ -528,7 +691,9 @@ def schedule(ops, opt):
                     dep.add(o2["id"])
         for a, w in acc:
             hist.setdefault(a["n"], []).append((op, a, w))
+        dep |= set(op.get("lag", ()))
         op["dep"] = dep
+        op["dep0"] = set(dep)
         op["tiles"] = set(a["n"] for a, w in acc if a["n"][:3] == "ps:")
     users = {}
     for op in ops:
@@ -538,7 +703,7 @@ def schedule(ops, opt):
     for op in ops:
         for d in op["dep"]:
             succ[d].append(op["id"])
-    X, SAME = 120.0, 80.0
+    X, SAME = opt["X"], opt["same"]
     for op in reversed(ops):
         op["pr"] = op["c"] + op.get("lat", 0) + max([ops[s]["pr"] + X for s in succ[op["id"]]] + [0])
     free = dict((e, 0.0) for e in "VSPQY")
@@ -547,59 +712,17 @@ def schedule(ops, opt):
     bank_of, tenant, order = {}, [None] * 8, []
     done = set()
 
+    def gap(a, b):
+        if a.get("id") in b.get("lag", ()):
+            return 0
+        return a.get("lat", 0) + (0 if a["e"] == b["e"] == "P" else SAME if a["e"] == b["e"] and "lat" not in a else X)
+
     def avail(op, extra=()):
         t = 0.0
         for d in list(op["dep"]) + list(extra):
-            o = ops[d]
-            t = max(t, o["end"] + (0 if o["e"] == op["e"] == "P" else SAME if o["e"] == op["e"] and "lat" not in o else X))
+            t = max(t, ops[d]["st"] + ops[d]["c"] + gap(ops[d], op))
         return t
-    base = np.array([op["pr"] for op in ops])
-    chs = np.array([op["ch"] for op in ops])
-    pr = base + opt["bias"] * (chs == 0)
-    for seed in opt["steps"]:
-        rs = np.random.RandomState(seed)
-        mid, wid, amp = rs.rand() * base.max(), 300 + rs.rand() ** 2 * 8000, rs.randn() * 2500
-        pr = pr + amp * ((np.abs(base - mid) < wid) & (chs == rs.randint(NCH)) & (rs.rand(len(ops)) < rs.choice([0.3, 1.0])))
-    pr = [float(x) for x in pr]
-
-    def gap(a, b):
-        return a.get("lat", 0) + (0 if a["e"] == b["e"] == "P" else SAME if a["e"] == b["e"] and "lat" not in a else X)
-    fw = [[(d, gap(ops[d], op)) for d in op["dep"]] for op in ops]
-    bw = [[(s, gap(op, ops[s])) for s in succ[op["id"]]] for op in ops]
-
-    def serial(key, pre, post, tail):
-        busy = dict((e, []) for e in "VSPQY")
-        n = [len(x) for x in pre]
-        rdy = [(key[i], i) for i in range(len(ops)) if not n[i]]
-        end = [0.0] * len(ops)
-        while rdy:
-            j = min(rdy)
-            rdy.remove(j)
-            i = j[1]
-            t = max([end[d] + g for d, g in pre[i]] + [ops[i].get("lat", 0) if tail else 0])
-            c, b = ops[i]["c"], busy[ops[i]["e"]]
-            k = len(b)
-            while k > 0 and b[k - 1][1] > t:
-                k -= 1
-            while k < len(b) and b[k][0] < t + c:
-                t = max(t, b[k][1])
-                k += 1
-            b.insert(k, (t, t + c))
-            end[i] = t + c
-            for s, g in post[i]:
-                n[s] -= 1
-                if not n[s]:
-                    rdy.append((key[s], s))
-        return end
-    if opt["fbi"]:
-        key = [-x for x in pr]
-        for it in range(opt["fbi"]):
-            e1 = serial(key, fw, bw, False)
-            e2 = serial([-x for x in e1], bw, fw, True)
-            key = [-x for x in e2]
-        e1 = serial(key, fw, bw, False)
-        top = max(e2)
-        pr = [-(e1[i] - ops[i]["c"]) * (1 - opt["mix"]) - (top - e2[i]) * opt["mix"] for i in range(len(ops))]
+    pr = [op["pr"] + opt["bias"] * (op["ch"] == 0) for op in ops]
     while ready:
         cand = []
         for i in ready:
@@ -616,11 +739,8 @@ def schedule(ops, opt):
             cand.append((st, i, op, new, pick, extra))
         first = min(cand, key=lambda x: x[:2])
         lim = first[0] + opt["th"] * first[2]["c"] + 30
-        if opt["th"] < 0:
-            st, i, op, new, pick, extra = max(cand, key=lambda x: (pr[x[1]], -x[1]))
-        else:
-            st, i, op, new, pick, extra = max([x for x in cand if x[2]["e"] == first[2]["e"] and x[0] <= lim],
-                                              key=lambda x: (pr[x[1]], -x[1]))
+        st, i, op, new, pick, extra = max([x for x in cand if x[2]["e"] == first[2]["e"] and x[0] <= lim],
+                                          key=lambda x: (pr[x[1]], -x[1]))
         if new:
             bank_of[new[0]] = pick
             tenant[pick] = new[0]
@@ -635,24 +755,42 @@ def schedule(ops, opt):
             left[s] -= 1
             if left[s] == 0:
                 ready.append(s)
+    net = network(ops, gap)
+    perm = improve(net, [op["id"] for op in order], opt)
+    res = replay(net, perm, [fresh(net)], 0)
+    order, bank_of, tenant = [ops[i] for i in perm], {}, [None] * 8
+    for op in order:
+        op["dep"] = set(op["dep0"]) - set(op.get("lag", ()))
+        op["st"] = res[3][op["id"]] - op["c"]
+        op["end"] = res[3][op["id"]] + op.get("lat", 0)
+        for t in op["tiles"]:
+            if t not in bank_of:
+                b = bank_of[t] = res[4][net["tile"][op["id"]]]
+                op["dep"] |= set(users.get(tenant[b], ()))
+                tenant[b] = t
     cnt = dict((e, 0) for e in "VSPQ")
     for op in order:
         if "sem" not in op:
             cnt[op["e"]] += 1
             op["sig"] = (op["e"], cnt[op["e"]])
         else:
-            op["sig"] = (op["sem"], 16)
+            op["sig"] = (op["sem"], 16 if op["ins"][0][0] == "dma" else 2 * opt["eng"])
     seen = dict((e, {}) for e in "VSPQY")
     for op in order:
         need = {}
         for d in op["dep"]:
             s, v = ops[d]["sig"]
-            if ops[d]["e"] == "P" and op["e"] == "P":
-                continue
-            need[s] = max(need.get(s, 0), v)
-        op["waits"] = [(s, v) for s, v in need.items() if seen[op["e"]].get(s, 0) < v]
-        for s, v in op["waits"]:
-            seen[op["e"]][s] = v
+            if not ops[d]["e"] == "P" == op["e"] and need.get(s, (0, 0))[0] < v:
+                need[s] = (v, d)
+        mine = seen[op["e"]]
+        op["waits"] = []
+        for s, (v, d) in sorted(need.items(), key=lambda x: -ops[x[1][1]]["end"]):
+            if mine.get(s, 0) < v:
+                op["waits"].append((s, v))
+                mine[s] = v
+                for s2, v2 in ops[d]["known"].items() if opt["clock"] else ():
+                    mine[s2] = max(mine.get(s2, 0), v2)
+        op["known"] = dict(mine)
     return order, bank_of, cnt
 
 
@@ -683,7 +821,7 @@ def bits(engines):
 
 def rank_program(g, core, T, topo):
     order, bank_of, cnt = plan()
-    n = len(T.cores)
+    n, ne = len(T.cores), OPT["eng"]
     msgs = [op["ins"][0][1][2] for op in order if op["ins"][0][0] == "xfer"]
     rank = T.rank_of(core)
     if rank is None:
@@ -693,12 +831,12 @@ def rank_program(g, core, T, topo):
                 if helper_of(src, dst, T, topo) != core:
                     continue
                 rid, pid = topo.addr(dst, core)
-                eng = topo.engines(core, dst)[:8]
+                eng = topo.engines(core, dst)[:ne]
                 for u in msgs:
-                    g.wait_ge(T.sem["h" + u], 8)
+                    g.wait_ge(T.sem["h" + u], ne)
                     buf = T["R" + u][:, lo:hi]
                     g.remote_dma(buf, buf, T.sem["h" + u], T.sem.sent, pid, rid, bits(eng))
-                g.wait_ge(T.sem.sent, len(eng) * len(msgs))
+                g.wait_ge(T.sem.sent, ne * len(msgs))
         return
     Q = {"V": g.vector, "S": g.scalar, "P": g.tensor, "Q": g, "Y": g.sync}
 
@@ -722,7 +860,7 @@ def rank_program(g, core, T, topo):
                 tr, used = [], []
                 for side, (lo, hi), s0 in ((-1, (1152, 1280), 0), (1, (0, 128), 64)):
                     to = helper_of(core, T.cores[(rank + side) % n], T, topo)
-                    eng = [e for e in topo.engines(core, to) if e not in used][:8]
+                    eng = [e for e in topo.engines(core, to) if e not in used][:ne]
                     used.extend(eng)
                     rid, pid = topo.addr(to, core)
                     tr.append(RemoteDMATransfer(dst_ids=[DstId(rid=rid, pnc=pid)], dma_engine_mask=bits(eng),
@@ -734,8 +872,8 @@ def rank_program(g, core, T, topo):
                 continue
             if kind == "dma":
                 o, i = args[2]
-                o = real(o) if isinstance(o, dict) else T[o[0]][:, o[1]:o[1] + 64]
-                i = real(i) if isinstance(i, dict) else T[i[0]][:]
+                o = real(o) if isinstance(o, dict) else T[o[0]][:, o[1]:o[2]]
+                i = real(i) if isinstance(i, dict) else T[i[0]][:] if len(i) == 1 else T[i[0]][:, i[1]:i[2]]
                 q.dma_start(o, i).then_inc(T.sem[op["sem"]], 16)
                 continue
             a = [real(x) for x in args]
@@ -769,5 +907,5 @@ def rank_program(g, core, T, topo):
     for s in DMAS:
         g.wait_ge(T.sem[s], 16)
     for u in msgs:
-        g.wait_ge(T.sem["h" + u], 16)
-    g.wait_ge(T.sem.sent, 16 * len(msgs))
+        g.wait_ge(T.sem["h" + u], 2 * ne)
+    g.wait_ge(T.sem.sent, 2 * ne * len(msgs))

import math
import numpy as np
from concourse.bass import DstId, RemoteDMATransfer
from concourse.mybir import dt, AluOpType, AxisListType, ActivationFunctionType
A = AluOpType
F = ActivationFunctionType

W, RO, NCH = 1536, 3, 2
H16, B16, F32, I32, U16 = "float16", "bfloat16", "float32", "int32", "uint16"
MAGIC = 1.5 * 2.0 ** 23
OPT = {"gam": 1.56, "pe": 0.42, "lat": 6500.0, "bias": 3000.0, "th": 0.0, "X": 300.0, "same": 150.0, "en": "SS",
       "tries": 22000, "seed": 1, "hot": 500.0, "cold": 20.0,
       "pa": "VS", "rc": "SS", "d": "QQ", "dl": "VVVV", "u16": "S", "cvt": "V", "eng": 8,
       "g": "VV", "nq": 4, "st2": True, "py2": True, "clock": True}

SCRATCH = {
    "X": ("sbuf", [128, W], B16), "G": ("sbuf", [128, W], B16), "EN": ("sbuf", [128, 2 * W], I32),
    "PK": ("sbuf", [128, W], F32),
    "e96": ("sbuf", [128, 96], I32), "ehl": ("sbuf", [128, 192], I32), "lin": ("sbuf", [128, 2, 192], I32),
    "BO": ("sbuf", [128, 128], F32), "IF": ("sbuf", [128, 128], F32), "SH": ("sbuf", [128, 512], F32),
    "LT": ("sbuf", [128, 128], F32), "BOh": ("sbuf", [128, 128], B16),
    "ID": ("sbuf", [128, 896], H16), "BC": ("sbuf", [128, 2048], B16), "DG": ("sbuf", [128, 2048], B16),
    "MD": ("sbuf", [128, 256], H16), "UH": ("sbuf", [128, 144], H16), "UE": ("sbuf", [128, 432], H16),
    "BO8": ("sbuf", [128, 8], F32), "PMI": ("sbuf", [128, 128], F32), "ONE": ("sbuf", [128, 128], H16),
    "pi": ("sbuf", [128, 8], I32), "col": ("sbuf", [128, 16], F32), "MK": ("sbuf", [128, 32], F32),
    "q4": ("sbuf", [128, 512], F32), "WZ": ("sbuf", [128, 896], H16),
    "WC": ("sbuf", [128, 128], B16), "WH": ("sbuf", [128, 192], B16), "WL": ("sbuf", [128, 256], B16),
    "NB": ("sbuf", [128, 320], F32), "VE": ("sbuf", [128, 144], H16),
}
for _c in range(NCH):
    for _n, _w, _t in (("abl", 192, H16), ("cn", 256, H16), ("ol", 192, U16), ("ot", 64, U16), ("ou", 128, U16),
                       ("Pa", 1024, F32), ("Pd", 1024, F32), ("d", 1024, I32), ("Rc", 1040, H16), ("gs", 1024, H16),
                       ("en", 2048, H16), ("t", 1024, H16), ("PP", 4096, F32),
                       ("xw", 1024, B16), ("dl", 1040, B16), ("ad", 1024, H16),
                       ("sh", 1536, H16), ("sf", 640, F32), ("si", 512, I32), ("bd", 512, H16), ("pay", 256, F32),
                       ("res", 192, F32), ("eb", 320, H16), ("oe", 16, U16), ("ee", 256, H16)):
        SCRATCH["%s%d" % (_n, _c)] = ("sbuf", [128, _w], _t)
    SCRATCH["so%d" % _c] = ("sbuf", [128, 192, 16], F32)
    SCRATCH["tq%d" % _c] = ("sbuf", [128, 32, 16], F32)
    for _r in range(RO):
        SCRATCH["R%d%d" % (_c, _r)] = ("sbuf", [128, 1280], F32)
        SCRATCH["S%d%d" % (_c, _r)] = ("sbuf", [128, 192], F32)
for _b in range(8):
    SCRATCH["bank%d" % _b] = ("psum", [128, 512], F32)

DMAS = ["lx", "lg", "ln", "le", "la", "lb", "ll", "eh", "el"] + ["o%d%d" % (c, q) for c in range(NCH) for q in range(3)]
SEMAPHORES = ["V", "S", "P", "Q", "sent"] + DMAS + ["h%d%d" % (c, r) for c in range(NCH) for r in range(RO)]


def ap(name, c0, c1, st=1, p0=0, p1=128):
    m = 0
    if st == 1:
        m = ((1 << (c1 - c0)) - 1) << c0
    else:
        for c in range(c0, c1, st):
            m |= 1 << c
    return {"n": name, "i": (slice(p0, p1), slice(c0, c1, st)), "p": (p0, p1), "m": m, "w": len(range(c0, c1, st))}


def ap3(name, r0, r1, rs, k0, k1):
    inner = SCRATCH[name][1][2]
    m = 0
    for r in range(r0, r1, rs):
        m |= ((1 << (k1 - k0)) - 1) << (inner * r + k0)
    rows = r0 if len(range(r0, r1, rs)) == 1 else slice(r0, r1, rs)
    idx = (slice(0, 128), rows, k0 if k1 - k0 == 1 else slice(k0, k1))
    return {"n": name, "i": idx, "p": (0, 128), "m": m, "w": len(range(r0, r1, rs)) * (k1 - k0)}


def ind(win, off):
    return {"win": win, "off": off, "w": 16 * off["w"]}


def two(a):
    return "n" in a and a["n"][:3] != "ps:" and SCRATCH[a["n"]][2] in (H16, B16, U16)


def build(opt):
    ops = []
    cy = 0.83
    cur = [-1]

    def add(eng, ins, cost, **kw):
        rd, wr = [], []
        for kind, args in ins:
            aps = [x for x in args if isinstance(x, dict)]
            wr.append(aps[0])
            for x in aps[1:]:
                rd.extend([x["win"], x["off"]] if "win" in x else [x])
        op = {"e": eng, "ins": ins, "c": cost, "rd": rd, "wr": wr, "id": len(ops), "ch": cur[0]}
        op.update(kw)
        ops.append(op)
        return op

    def vcost(out, x, n2):
        if "win" in x:
            return 50 + x["w"] * opt["gam"] * cy
        return max(64, x["w"] * n2) * cy

    def tt(out, x, y, o):
        ps = "win" not in x and (x["n"][:3] == "ps:" or y["n"][:3] == "ps:")
        add("V", [("tt", (out, x, y, o))], vcost(out, x, 1 if ps else 2))

    def ts(out, x, s1, o1, s2=None, o2=None):
        add("V", [("ts", (out, x, s1, s2, o1, o2))], vcost(out, x, 0.5 if two(out) and two(x) else 1))

    def cp(out, x):
        add("V", [("cp", (out, x))], vcost(out, x, 0.5 if two(out) and two(x) else 1))

    def ms(out, v):
        add("V", [("ms", (out, v))], vcost(out, out, 0.5 if two(out) else 1))

    def act(out, x, f=F.Copy, scale=1.0, bias=0.0):
        c = 65 + x["w"] * opt["gam"] * cy if "win" in x else max(64, x["w"]) * cy
        add("S", [("act", (out, x, f, bias, scale))], c)

    def lin(out, x, scale, bias):
        act(out, x, F.Identity if bias else F.Copy, scale, bias)

    def offs(out, x):
        if opt["u16"] == "S":
            act(out, x)
        else:
            cp(out, x)

    def mm(lst, after=None):
        c = 0
        for out, l, r, s, e in lst:
            c += max(min(64, l["w"]), r["w"]) * (1 if two(r) else 4) * opt["pe"]
        op = add("P", [("mm", x) for x in lst], c)
        if after:
            op["after"] = after

    def grp(out, terms, first=True, last=True):
        return [(out, l, r, first and i == 0, last and i == len(terms) - 1) for i, (l, r) in enumerate(terms)]

    def sel(out, x, pat, o, base, cm):
        add("Q", [("sel", (out, x, pat, o, 0.0, base, cm))], 170 + 2 * cy * out["w"])

    def iota(out, pat, base, cm):
        add("Q", [("iota", (out, pat, base, cm))], 130 + 2 * cy * out["w"])

    def conv(e, out, x):
        if e == "S":
            act(out, x)
        else:
            sel(out, x, [[0, out["w"]]], A.is_ge, 0, 0)

    def dma(q, sem, out, src, lat):
        o = {"n": "hbm", "p": (0, 0), "m": 0, "w": 0}
        add(q, [("dma", (out if isinstance(out, dict) else o, src if isinstance(src, dict) else o, (out, src)))], 60,
            sem=sem, lat=lat)

    for sem, o, n, lat in (("le", ap("e96", 0, 96), "erec", 2300), ("lx", ap("X", 0, W), "xrec", 3600),
                           ("lg", ap("G", 0, W), "grec", 4600), ("ln", ap("EN", W, 2 * W), "nbr", 6600)):
        dma("Y", sem, o, (n,), lat)
        if sem != "le":
            ops[-1]["lag"] = [ops[-2]["id"]]
    for q, (sem, n) in enumerate((("la", "pa"), ("lb", "pb"), ("ll", "lam"))):
        dma("S", sem, ap3("lin", 0, 2, 1, 64 * q, 64 * q + 64), (n,), 2800)
    ms(ap("EN", 0, W), 0)
    ts(ap("ehl", 0, 96), ap("e96", 0, 96), 10, A.logical_shift_right)
    ts(ap("ehl", 96, 192), ap("e96", 0, 96), 1023, A.bitwise_and)
    for q, sem in ((0, "eh"), (1, "el")):
        o = ap("EN", 0, W)
        o["i"] = (slice(q, 128, 16), slice(0, W))
        o["nowaw"] = True
        dma("Y", sem, o, ap("ehl", 96 * q, 96 * q + 96), 2200)

    BO, IF = ap("BO", 0, 128), ap("IF", 0, 128)
    ms(BO, 1.0)
    ms(IF, 1.0)
    iota(ap("pi", 0, 1), [[0, 1]], 0, 1)
    iota(ap("MK", 16, 32), [[1, 16]], 0, 0)
    sel(IF, IF, [[-1, 128]], A.is_equal, 0, 1)
    sel(BO, BO, [[-16, 8], [0, 16]], A.is_ge, 0, 1)
    sel(BO, BO, [[16, 8], [0, 16]], A.is_ge, 15, -1)
    ts(ap("pi", 4, 5), ap("pi", 0, 1), 15, A.bitwise_and)
    cp(ap("col", 0, 1), ap("pi", 4, 5))
    ts(ap("MK", 0, 16), ap("MK", 16, 32), ap("col", 0, 1), A.is_equal)
    I1, IG, IN, IM8, IK, IM2 = [ap("ID", 128 * i, 128 * i + 128) for i in range(6)]
    act(I1, IF)
    for o, v in ((IG, 2.0 ** -12), (IN, -1.0), (IM8, -8.0), (IK, float(W)), (IM2, -2.0)):
        ts(o, I1, v, A.mult)
    for j in range(3):
        o, p = 512 * j, ap("ps:pk%d" % j, 0, 512)
        mm([(p, I1, ap("X", o, o + 512), True, False)])
        mm([(p, IG, ap("G", o, o + 512), False, True)])
        if j == 1:
            ts(ap("PK", o, o + 512), p, 8.0, A.mult, 1028.0, A.add)
        else:
            lin(ap("PK", o, o + 512), p, 8.0, 1028.0)
    lin(ap("BOh", 0, 128), BO, 0.125, 0.0)
    for k in range(16):
        ts(ap("BC", 128 * k, 128 * k + 128), ap("BOh", 0, 128), ap("MK", k, k + 1), A.mult)
        act(ap("DG", 128 * k, 128 * k + 128), IF, F.Copy, ap("MK", k, k + 1))
    m0c, m15 = ap("MK", 0, 1), ap("MK", 15, 16)
    ts(ap("col", 1, 2), m0c, 1024.0, A.mult, ap("MK", 1, 2), A.add)
    ts(ap("col", 2, 3), m15, -1.0, A.mult, 1.0, A.add)
    ts(ap("col", 3, 4), m0c, m15, A.add)
    ts(ap("col", 4, 5), ap("col", 0, 1), 2.0, A.add)
    n15 = ap("col", 2, 3)
    ms(ap("UH", 0, 144), 0.0)
    ms(ap("UE", 0, 432), 0.0)
    ms(ap("VE", 0, 144), 0.0)
    ms(ap("ONE", 0, 64), 1.0)
    ms(ap("ONE", 64, 128), 2048.0)
    B8 = ap("BO", 0, 128, 16)
    ts(ap("UH", 15, 128, 16), B8, 1.0 / 128, A.mult)
    for i, v in enumerate((1.0, -1.0, 8.0)):
        ts(ap("UE", 144 * i + 15, 144 * i + 128, 16), B8, ap("col", 1, 2), A.mult, v, A.mult)
    ts(ap("VE", 15, 128, 16), B8, m0c, A.mult)
    ts(ap("VE", 17, 130, 16), B8, m15, A.mult)
    act(ap("BO8", 0, 8), B8)
    lin(ap("PMI", 0, 128), IF, -1.0, 0.0)
    M1, MN = ap("MD", 0, 128), ap("MD", 128, 256)
    ts(M1, I1, ap("col", 3, 4), A.mult)
    ts(MN, IN, ap("col", 3, 4), A.mult)
    sel(ap("SH", 384, 512), BO, [[-1, 128]], A.is_equal, -1, 1)
    sel(ap("SH", 0, 128), BO, [[-1, 128]], A.is_equal, 1, 1)
    sel(ap("SH", 128, 256), BO, [[-1, 128]], A.is_equal, -15, 1)
    sel(ap("SH", 256, 384), BO, [[-1, 128]], A.is_equal, 15, 1)
    sel(ap("LT", 0, 128), BO, [[1, 128]], A.is_gt, 0, -1)
    tt(ap("SH", 0, 128), ap("SH", 384, 512), ap("SH", 0, 128), A.subtract)
    lin(ap("SH", 0, 128), ap("SH", 0, 128), 4096.0, 0.0)
    lin(ap("SH", 128, 256), ap("SH", 128, 256), -4096.0, 0.0)
    lin(ap("SH", 256, 384), ap("SH", 256, 384), 4096.0, 0.0)
    PRV, NXT, NA, NBB, NW = [ap("NB", 64 * i, 64 * i + 64) for i in range(5)]
    iota(NA, [[16, 64]], 63, 0)
    iota(NBB, [[15, 64]], 63, 0)
    ts(NW, NBB, m0c, A.mult, ap("col", 0, 1), A.subtract)
    tt(PRV, NA, NW, A.subtract)
    lin(NBB, NBB, -1.0, 1071.0)
    ts(NW, NBB, m15, A.mult, ap("col", 4, 5), A.add)
    tt(NXT, NA, NW, A.add)
    EQ, EQ1, L4, M4, IR, WK, WQ = [ap("q4", 64 * i, 64 * i + 64) for i in range(7)]
    tt(EQ, ap("IF", 0, 64), ap("IF", 64, 128), A.add)
    tt(EQ1, ap("SH", 384, 448), ap("SH", 448, 512), A.add)
    tt(L4, ap("LT", 0, 64), ap("LT", 64, 128), A.add)
    tt(M4, ap("BO", 0, 64), ap("BO", 64, 128), A.add)
    iota(IR, [[0, 4], [1, 16]], 0, 0)
    tt(IR, IR, M4, A.mult)
    lin(ap("WC", 0, 64), EQ, 2.0 ** -18, 0.0)
    lin(ap("WC", 64, 128), EQ1, 2.0 ** -26, 0.0)
    lin(ap("WH", 0, 64), EQ, 2.0 ** -15, 0.0)
    lin(WQ, L4, 2.0, 0.0)
    tt(WQ, WQ, EQ, A.add)
    lin(ap("WH", 64, 128), WQ, 15 * 2.0 ** -19, 0.0)
    lin(ap("WL", 128, 192), WQ, 15 * 2.0 ** -19, 0.0)
    ts(ap("WH", 128, 192), IR, 2.0 ** -18, A.mult, n15, A.mult)
    ms(ap("WH", 143, 192, 16), 0.0)
    act(ap("WL", 192, 256), ap("WH", 128, 192))
    ts(ap("WL", 64, 128), IR, 0.125, A.mult, m15, A.mult)
    ts(WK, EQ, 2.0 ** -19, A.mult, n15, A.mult)
    tt(ap("WL", 0, 64), WK, ap("WL", 64, 128), A.add)
    wz0, wz1 = ap("ps:wz", 0, 64), ap("ps:wz", 64, 128)
    ts(wz0, M4, 4.0, A.mult, m15, A.mult)
    lin(WK, L4, -1920.0, 0.0)
    tt(WK, WK, wz0, A.add)
    ts(wz1, M4, 128.0, A.mult, n15, A.mult)
    for k in range(14):
        tt(ap("WZ", 64 * k, 64 * k + 64), WK if k == 0 else ap("WZ", 64 * k - 64, 64 * k), wz1, A.add)

    Xw, Pw = ap("X", 0, W), ap("PK", 0, W)
    for c in range(NCH):
        cur[0] = c
        s = str(c)

        def a_(n, c0, c1, st=1, p0=0, p1=128):
            return ap(n + s, c0, c1, st, p0, p1)

        def sh(i, n=1, p0=0, p1=128):
            return a_("sh", 64 * i, 64 * (i + n), 1, p0, p1)

        def sf(i, n=1):
            return a_("sf", 64 * i, 64 * (i + n))

        def si(i, n=1):
            return a_("si", 64 * i, 64 * (i + n))

        def eb(i, n=1):
            return a_("eb", 64 * i, 64 * (i + n))
        ra, rb, rl = a_("abl", 0, 64), a_("abl", 64, 128), a_("abl", 128, 192)
        av, bv, lv, l8 = [a_("cn", 64 * i, 64 * i + 64) for i in range(4)]
        ms(a_("bd", 0, 512), 0.0)
        ms(ap3("tq" + s, 0, 32, 1, 0, 16), 0.0)
        for k in (0, 15):
            ms(ap3("so" + s, 14, 64, 16, k, k + 1), 0.0)
            ms(ap3("so" + s, 78, 128, 16, k, k + 1), 2.0 ** -15)
            ms(ap3("so" + s, 142, 192, 16, k, k + 1), 1920 * 2.0 ** -26)
        act(a_("abl", 0, 192), ap3("lin", c, c + 1, 1, 0, 192))
        st2 = "su" if opt["st2"] else "st"
        mm(grp(ap("ps:%s%s0" % (st2, s), 192, 256), [(I1, rb), (IN, ra)]))
        for r in range(RO):
            u, un = s + str(r), s + str(r + 1)

            def ps(n, c0, c1, st=1, p0=0, p1=128):
                return ap("ps:" + n + u, c0, c1, st, p0, p1)

            def cn(i, n=1, p0=0, p1=128):
                return ps("cn", 64 * i, 64 * (i + n), 1, p0, p1)

            def send(v):
                add("Q", [("xfer", (ap("R" + v, 0, 128), ap("S" + v, 0, 192), v)), ("none", (ap("R" + v, 1152, 1280),))],
                    1000, sem="h" + v, lat=opt["lat"])
            Rw, Sd = "R" + u, "S" + u
            m8, pas = sh(18 + r), sh(21 + r)
            m0, md8, md0, zz, sp, sn, spd, sq2, sq1, pd, cm = [sh(i) for i in (0, 1, 2, 3, 4, 5, 6, 7, 11, 12, 13)]
            lsrc = rl if r == 0 else ps(st2, 128, 192)
            if opt["st2"]:
                ts(m8, lsrc, 7.5, A.is_ge)
                ts(m0, lsrc, 0.5, A.is_lt)
            else:
                act(m8, lsrc, F.Relu, 1.0, -7.0)
                act(m0, lsrc, F.Relu, -1.0, 1.0)
            if r:
                act(a_("abl", 0, 192), ps("st", 0, 192))
            tt(md8, m8, ps(st2, 192, 256), A.mult)
            tt(md0, m0, ps(st2, 192, 256), A.mult)
            mm(grp(cn(1), [(I1, ra), (I1, md8)]) + grp(cn(2), [(I1, rb), (IN, md8)]) +
               grp(cn(0), [(I1, rb), (IK, m8), (IK, m0), (IN, md0)]) + grp(cn(3), [(I1, rl), (IM8, m8)]))
            offs(a_("ol", 0, 192), cn(0, 3))
            act(a_("cn", 0, 192), cn(1, 3))
            mm(grp(cn(4), [(I1, bv), (IN, av), (I1, md8), (IN, md0)]) + grp(cn(5), [(I1, bv), (IN, av)]))
            on, oa, ob = 0, 64, 128
            for h in range(2):
                o = 512 * h
                (act if opt["pa"][h] == "S" else cp)(a_("Pa", o, o + 512), ind(Pw, a_("ol", oa + 32 * h, oa + 32 * h + 32)))
                tt(a_("Pd", o, o + 512), ind(Pw, a_("ol", ob + 32 * h, ob + 32 * h + 32)), a_("Pa", o, o + 512), A.subtract)
            late = r == 0
            for h in range(2):
                lb_, vs = ps("L%d" % h, 0, 512), ap(Rw, 128 + h, 1152, 2)
                mm([(ps("L%d" % h, j, 512, 8), ap("BC", 128 * (2 * j + h), 128 * (2 * j + h) + 128), lv, True, True)
                    for j in range(8)])
                if late:
                    e = ap(Sd, 128 * h, 128 * h + 64)
                    tt(e, a_("Pd", 15 * h, 1024, 16), ps("L%d" % h, 7 * h, 512, 8), A.mult)
                    tt(e, e, a_("Pa", 15 * h, 1024, 16), A.add)
                tt(lb_, a_("Pd", h, 1024, 2), lb_, A.mult)
                tt(vs, a_("Pa", h, 1024, 2), lb_, A.add)
                conv(opt["rc"][h], a_("Rc", h, 1024, 2), vs)

            def half(n, h, o=0):
                return ap(n, o + 512 * h, o + 512 * h + 512)

            def prod(q, h):
                return half("PP" + s, h, 1024 * q)

            def total(q):
                mm([(ps("s%d" % q, j, 64, 8), a_("PP", 1024 * q + j, 1024 * q + 1024, 8), ap("BO8", 0, 8), True, True)
                    for j in range(8)])
                if q % 2 == 0:
                    act(sf(4 + q // 2), ps("s%d" % q, 0, 64))
                    return
                for j in range(2):
                    o = 8 * (q - 1 + j)
                    tt(ap3("tq" + s, o, o + 8, 1, 8 * j, 8 * j + 8), sf(4 + q // 2), ps("s%d" % q, 0, 64), A.mult)
                mm(grp(ps("df", 0, 64), [(ap3("tq" + s, 8 * (q - 1 + j), 8 * (q + j), 1, 0, 16),
                                          ap("PMI", j, 128, 2) if q == 1 else ap("IF", j, 128, 2)) for j in range(2)], q == 1, q == 3))
            for h in range(2):
                gb = ps("g%d" % h, 0, 512)
                conv(opt["d"][h], half("d" + s, h), half("Pd" + s, h))
                if opt["g"][h] == "P":
                    mm([(gb, IF, half(Rw, h, 128), True, False)])
                    mm([(gb, IN, half("Rc" + s, h), False, True)])
                    act(half("gs" + s, h), gb)
                else:
                    mm([(ps("r%d" % h, 0, 512), I1, half("Rc" + s, h), True, True)])
                    tt(half("gs" + s, h), half(Rw, h, 128), ps("r%d" % h, 0, 512), A.subtract)
                    mm([(gb, I1, half("gs" + s, h), True, True)], half("d" + s, h))
                tt(prod(0, h), half("d" + s, h), gb, A.mult)
            total(0)
            lin(l8, lv, -1.0, 8.0)
            act(zz, lv, F.Relu, -1.0, 1.0)
            for h in range(2):
                (act if opt["en"][h] == "S" else cp)(a_("en", 512 * h, 512 * h + 512),
                                                     ind(ap("EN", 0, W), a_("ol", oa + 32 * h, oa + 32 * h + 32)))
            act(a_("en", 1024, 2048), ind(ap("EN", 0, 2 * W), a_("ol", on, on + 64)))
            for q in range(2):
                mm(grp(ps("E", 64 * q, 64 * q + 64),
                       [(ap("UE", 15 - k, 143 - k), a_("en", 1024 * q + k, 1024 * q + 1024, 16)) for k in range(16)]))
                tt(sf(q), ps("E", 64 * q, 64 * q + 64), (l8, lv)[q], A.mult)
            if late:
                tt(ap(Sd, 64, 128), sf(0), sf(1), A.add)
                send(u)
            mm(grp(cn(6), [(ap("DG", 128 * k, 128 * k + 128), a_("en", 1024 + k, 2048, 16)) for k in range(16)] + [(IN, av)]))
            tt(cn(6), zz, cn(6), A.mult)
            for h in range(2):
                o = 64 * h
                act(a_("bd", 384 + o, 448 + o, 1, o, o + 64), a_("cn", 0, 64, 1, o, o + 64))
            ed = ps("ed", 0, 64)
            halo = [(ap("SH", 128, 256), ap(Rw, 0, 64)), (ap("SH", 256, 384), ap(Rw, 1216, 1280))]
            own = [(ap("SH", 0, 128), sf(1))]
            mm(grp(ed, [(I1, ap("ONE", 64, 128)), (ap("SH", 0, 128), sf(0))] + (own if late else halo), True, False))
            mm(grp(ed, halo if late else own, False, True))
            tt(ed, ed, PRV, A.max)
            tt(ed, ed, NXT, A.min)
            offs(a_("ot", 0, 64), ed)
            for h in range(2):
                o = 512 * h
                act(a_("t", o, o + 512), ind(ap(Rw, 64, 1216), a_("ot", 32 * h, 32 * h + 32)))
            for h in range(2):
                tb = ps("t%d" % h, 0, 512)
                mm(grp(tb, [(I1, half("t" + s, h)), (IN, half("Rc" + s, h))]))
                tt(prod(2, h), half("gs" + s, h), tb, A.mult)
                act(prod(1, h), tb, F.Square)
                tt(prod(3, h), half("d" + s, h), tb, A.mult)
            for q in (2, 1, 3):
                total(q)
            df = ps("df", 0, 64)
            ts(sp, df, 0.0, A.is_gt)
            ts(sn, df, 0.0, A.is_lt)
            tt(sq1, sn, cn(4), A.mult)
            tt(sh(6, 2), sh(4, 2), cn(5, 2), A.mult)
            mm(grp(cn(1), [(I1, av), (I1, sq1)]) + grp(cn(0), [(I1, av), (I1, spd), (I1, sq2)]) +
               grp(cn(7), [(I1, lv), (I1, sp), (IN, sn)]))
            offs(a_("ou", 0, 128), cn(0, 2))
            ts(cm, cn(7), 4.5, A.is_gt)
            for h in range(2):
                o = 64 * h
                tt(a_("bd", o, o + 64, 1, o, o + 64), sh(13, 1, o, o + 64), cn(5, 1, o, o + 64), A.mult)
            bn, ln = eb(0), eb(1)
            act(pas, cn(7), F.Relu, -1.0, 0.0)
            act(ln, cn(7), F.Abs)
            tt(pd, pas, cn(5), A.mult)
            mm(grp(cn(2), [(I1, bv), (I1, sq2), (IN, pd)]))
            act(bn, cn(2))
            nq = opt["nq"]
            wq, pq = 1024 // nq, 64 // nq
            for h in range(nq):
                o = wq * h
                act(a_("xw", o, o + wq), ind(Xw, a_("ou", 64 + pq * h, 64 + pq * h + pq)))
                if opt["dl"][h] == "V":
                    tt(a_("dl", o, o + wq), ind(Xw, a_("ou", pq * h, pq * h + pq)), a_("xw", o, o + wq), A.subtract)
                else:
                    (act if opt["dl"][h] == "S" else cp)(a_("dl", o, o + wq), ind(Xw, a_("ou", pq * h, pq * h + pq)))
            if r < RO - 1:
                Sn = "S" + un
                mm(grp(ps("cn", 192, 208), [(ap("VE", 15 - 4 * j, 143 - 4 * j), a_("eb", 16 * j, 16 * j + 16)) for j in range(4)]))
                offs(a_("oe", 0, 16), ps("cn", 192, 208))
                act(a_("ee", 0, 256), ind(ap("EN", 0, W), a_("oe", 0, 16)))
                e0, e15 = a_("en", 0, 1024, 16), a_("en", 15, 1024, 16)
                gr = grp(ps("eE", 64, 128), [(ap("UE", 303, 431), e0), (ap("UE", 288, 416), e15)])
                for j in range(4):
                    o = 256 * j
                    gr += grp(ps("eE", 16 * j, 16 * j + 16),
                              [(ap("UE", 159, 287), a_("en", o, o + 256, 16)), (ap("UE", 144, 272), a_("en", o + 15, o + 256, 16)),
                               (ap("UE", 15, 143), a_("ee", 4 * j, 256, 16)), (ap("UE", 0, 128), a_("ee", 4 * j + 2, 256, 16))])
                mm(gr)
                tt(sf(2), ln, ps("eE", 0, 64), A.mult)
                tt(ap(Sn, 64, 128), sf(2), ps("eE", 64, 128), A.add)
                gr = []
                for h in range(2):
                    n = 1 if len(set(opt["dl"][:nq])) == 1 else nq
                    for j in range(n):
                        o, e, p = 1024 // n * j + 15 * h, 1024 // n * (j + 1), 128 + 64 * h + 64 // n * j
                        gr += grp(ps("eE", p, p + 64 // n), [(I1, a_("Rc", o, e, 16)), (I1, a_("dl", o, e, 16))] +
                                  ([] if opt["dl"][j] == "V" else [(IN, a_("xw", o, e, 16))]))
                mm(gr)
                for h in range(2):
                    act(ap(Sn, 128 * h, 128 * h + 64), ps("eE", 128 + 64 * h, 192 + 64 * h))
                send(un)
                ea, ebb, el = [(0, av)], [(0, bn)], [(0, ln)]
            else:
                mm(grp(cn(3), [(I1, sh(18 + i)) for i in range(2 * RO)]))
                cp(si(7), cn(3))
                ts(si(7), si(7), 1, A.bitwise_and)
                mm(grp(cn(3), [(I1, bn), (IN, av)]) + grp(cn(4), [(IM2, ln)]))
                tt(eb(2), si(7), cn(3), A.mult)
                ts(cn(4), cn(4), 8.0, A.add)
                tt(eb(3), si(7), cn(4), A.mult)
                ea, ebb, el = [(0, av), (0, eb(2))], [(0, bn), (128, eb(2))], [(0, ln), (0, eb(3))]
            for h in range(nq):
                o, e = wq * h, wq * h + wq
                db, two_ = ps("D%d" % h, 0, wq - 1), opt["dl"][h] != "V"
                mm(grp(db, [(I1, a_("Rc", o + 1, e)), (IN, a_("Rc", o, e - 1))], True, False), a_("xw", o, e))
                if two_:
                    mm(grp(db, [(IN, a_("xw", o + 1, e)), (I1, a_("xw", o, e - 1))], False, False))
                mm(grp(db, [(I1, a_("dl", o + 1, e)), (IN, a_("dl", o, e - 1))], False, True))
                act(a_("ad", o, e - 1), db, F.Abs)
            mm(grp(ps("H", 0, 64), [(ap("UH", 0, 128), ap("ONE", 0, 64))] +
                   [(ap("UH", 15 - j, 143 - j), a_("ad", j, 1024, 16)) for j in range(15)]))
            for h in range(2):
                o = 64 * h
                ts(a_("bd", 128 + o, 192 + o, 1, o, o + 64), ps("H", 0, 64, 1, o, o + 64), MAGIC, A.add, -MAGIC, A.add)
            for h in range(2):
                o = 64 * h
                tt(a_("bd", 256 + o, 320 + o, 1, o, o + 64), ps("H", 0, 64, 1, o, o + 64),
                   a_("bd", 128 + o, 192 + o, 1, o, o + 64), A.subtract)
            cb, hb, lb, ab = [a_("bd", 128 * i, 128 * i + 128) for i in range(4)]
            g0 = [(cb, ap("WC", 0, 64)), (ab, ap("WC", 0, 64)), (lb, ap("WL", 0, 64))]
            rest = (grp(ps("py", 64, 128), [(cb, ap("WC", 64, 128)), (ab, ap("WC", 64, 128)), (lb, ap("WL", 64, 128)),
                                            (hb, ap("WH", 0, 64))]) +
                    grp(ps("py", 128, 256), [(lb, ap("WL", 128, 256)), (hb, ap("WH", 64, 192))]))
            if opt["py2"]:
                mm(grp(ps("px", 0, 64), g0))
                act(a_("pay", 0, 64), ps("px", 0, 64))
                mm(rest)
                act(a_("pay", 64, 256), ps("py", 64, 256))
            else:
                mm(grp(ps("py", 0, 64), g0) + rest)
                act(a_("pay", 0, 256), ps("py", 0, 256))
            for h in range(2):
                wz = ap("WZ", 448 * h, 448 * h + 448)
                mm(grp(ps("Z%d" % h, 0, 448), [(hb, wz), (lb, wz)]))
            for q in range(3):
                for h in range(2):
                    add("V", [("scan", (ap3("so" + s, 64 * q, 64 * q + 64, 1, 1 + 7 * h + j, 2 + 7 * h + j),
                                        ps("Z%d" % h, 64 * j, 64 * j + 64), a_("pay", 64 * q, 64 * q + 64)))
                              for j in range(7)], 7 * 64 * cy)
            gp, rc, y = sf(6), sf(7), sf(8)
            for q in range(2):
                x = ap3("so" + s, 64 * q + 14, 64 * q + 64, 16, 0, 16)
                if opt["cvt"] == "S" or q:
                    lin(si(q), x, 2.0 ** 26, 64.0 - 64 * q)
                else:
                    ts(si(q), x, 2.0 ** 26, A.mult, 64.0, A.add)
            ts(si(4), si(0), 255, A.bitwise_and)
            ts(si(5), si(1), 4, A.logical_shift_right, 127 * 128, A.bitwise_and)
            tt(gp, si(4), si(5), A.add)
            ts(gp, gp, -64.0, A.add, 1.0 / 240, A.max)
            add("V", [("rcp", (rc, gp))], 190 + 6 * 64 * cy)
            ts(si(2), si(0), 8, A.logical_shift_right, 2047, A.bitwise_and)
            ts(si(3), si(1), 2047, A.bitwise_and)
            act(sh(8, 2), si(2, 2))
            tt(y, a_("pay", 192, 256), ap3("so" + s, 142, 192, 16, 0, 16), A.subtract)
            lin(y, y, 2.0 ** 28 / 15, 1.0 / 60)
            tt(si(6), y, rc, A.mult)
            lin(sh(10), si(6), 1.0, 4.0)

            def turn(n, q, edge, terms):
                gr = []
                for o in (0, 64):
                    gr += grp(ap("ps:" + n + un, 64 * q, 64 * q + 64, 1, o, o + 64),
                              [(ap("MD", m + o, m + o + 64), x) for m, x in edge] +
                              [(sh(x, 1, o, o + 64), ap("ID", m + o, m + o + 64, 1, o, o + 64)) for x, m in terms])
                return gr
            mm(turn("st", 0, ea, [(8, 0)]) + turn("st", 1, ebb, [(9, 0)]))
            if r < RO - 1:
                mm(turn(st2, 3, [(0, bn), (128, av)], [(9, 0), (8, 256)]))
                if opt["st2"]:
                    mm(turn(st2, 2, el, [(10, 0)]))
            mm(turn("st", 2, el, [(10, 0)]))
            if r == RO - 1:
                act(a_("res", 0, 128), ap("ps:st" + un, 0, 128))
                act(a_("res", 128, 192), ap("ps:st" + un, 128, 192))
                for q, n in enumerate(("ya", "yb", "yl")):
                    dma("S" if q == 2 else "Y", "o%d%d" % (c, q), (n, 64 * c, 64 * c + 64), a_("res", 64 * q, 64 * q + 64), 2000)
    return ops


STEP = 24


def network(ops, gap):
    anc, pre, names = [], [], {}
    for op in ops:
        seen, keep = 0, []
        for d in sorted(op["dep0"], reverse=True):
            if not seen >> d & 1 or "lat" in ops[d]:
                keep.append((d, gap(ops[d], op)))
            seen |= anc[d] | 1 << d
        anc.append(seen)
        pre.append(keep)
    tile = [names.setdefault(min(op["tiles"]), len(names)) if op["tiles"] else -1 for op in ops]
    return {"anc": anc, "pre": pre, "tile": tile, "eng": ["VSPQY".index(op["e"]) for op in ops],
            "cost": [op["c"] for op in ops], "tail": [op.get("lat", 0) for op in ops],
            "uses": [tile.count(t) for t in range(len(names))], "X": gap({"e": "V"}, {"e": "S"})}


def fresh(net):
    n = len(net["pre"])
    return ([0.0] * n, [-1] * n, [0.0] * 5, [-1] * 5, net["uses"], [-1] * len(net["uses"]), [0.0] * 8, [-1] * 8,
            list(range(8)), 0.0, -1)


def replay(net, perm, marks, k0):
    pre, eng, cost, tail, tile, X = net["pre"], net["eng"], net["cost"], net["tail"], net["tile"], net["X"]
    m = marks[k0]
    end, why, free, lastop, left, bank, bfree, blast, avail = [list(x) for x in m[:9]]
    top, topi = m[9], m[10]
    marks = marks[:k0 + 1]
    for p0 in range(k0 * STEP, len(perm), STEP):
        if p0 > k0 * STEP:
            marks.append((end, why, list(free), list(lastop), list(left), list(bank), list(bfree), list(blast),
                          list(avail), top, topi))
        for i in perm[p0:p0 + STEP]:
            e = eng[i]
            t, w = free[e], lastop[e]
            for d, g in pre[i]:
                x = end[d] + g
                if x > t:
                    t, w = x, d
            tl = tile[i]
            if tl >= 0:
                b = bank[tl]
                if b < 0:
                    if not avail:
                        return None
                    b = avail[0]
                    for y in avail:
                        if bfree[y] < bfree[b]:
                            b = y
                    avail.remove(b)
                    bank[tl] = b
                    if bfree[b] > t:
                        t, w = bfree[b], blast[b]
                t += cost[i]
                if t + X > bfree[b]:
                    bfree[b], blast[b] = t + X, i
                left[tl] -= 1
                if not left[tl]:
                    avail.append(b)
            else:
                t += cost[i]
            end[i] = free[e] = t
            lastop[e] = i
            why[i] = w
            if t + tail[i] > top:
                top, topi = t + tail[i], i
    return top, topi, why, end, bank, marks


def improve(net, perm, opt):
    anc, n = net["anc"], opt["tries"]
    rnd = np.random.RandomState(opt["seed"]).rand(n, 4).tolist()
    cur = replay(net, perm, [fresh(net)], 0)
    best = (cur[0], perm)
    runs = None
    for it in range(n):
        if runs is None:
            i, why, runs, run = cur[1], cur[2], [], []
            while why[i] >= 0:
                if anc[i] >> why[i] & 1:
                    run = []
                else:
                    if not run:
                        run = [i]
                        runs.append(run)
                    run.append(why[i])
                i = why[i]
            pairs = [(r, j) for r in runs for j in range(len(r) - 1)]
        if not pairs:
            break
        a, b, c, d = rnd[it]
        r, j = pairs[int(a * len(pairs))]
        if b < 0.5:
            v, u = r[j], r[j + 1 if c < 0.5 else j + 1 + int((2 * c - 1) * (len(r) - j - 1))]
        else:
            u, v = r[j + 1], r[j if c < 0.5 else int((2 * c - 1) * (j + 1))]
        if anc[v] >> u & 1:
            continue
        pu = perm.index(u)
        pv = perm.index(v, pu)
        mid = perm[pu:pv + 1]
        if b < 0.5:
            s = anc[v] | 1 << v
            new = [x for x in mid if s >> x & 1] + [x for x in mid if not s >> x & 1]
        else:
            s = [x == u or anc[x] >> u & 1 for x in mid]
            new = [x for x, y in zip(mid, s) if not y] + [x for x, y in zip(mid, s) if y]
        new = perm[:pu] + new + perm[pv + 1:]
        res = replay(net, new, cur[5], pu // STEP)
        heat = opt["hot"] * (opt["cold"] / opt["hot"]) ** (it / n)
        if res and res[0] <= cur[0] - heat * math.log(d + 1e-12):
            cur, perm, runs = res, new, None
            if res[0] < best[0]:
                best = (res[0], new)
    return best[1]


def schedule(ops, opt):
    hist = {}
    for op in ops:
        dep = set()
        acc = [(a, False) for a in op["rd"]] + [(a, True) for a in op["wr"]]
        if "after" in op:
            acc.append((op["after"], False))
        for a, w in acc:
            if a["n"] == "hbm":
                continue
            isps = a["n"][:3] == "ps:"
            for (o2, a2, w2) in hist.get(a["n"], ()):
                if o2 is op:
                    continue
                if isps and (o2["e"] != op["e"] or op["e"] == "P"):
                    dep.add(o2["id"])
                elif (w or w2) and a["m"] & a2["m"] and a["p"][0] < a2["p"][1] and a2["p"][0] < a["p"][1]:
                    if "nowaw" in a and "nowaw" in a2:
                        continue
                    dep.add(o2["id"])
        for a, w in acc:
            hist.setdefault(a["n"], []).append((op, a, w))
        dep |= set(op.get("lag", ()))
        op["dep"] = dep
        op["dep0"] = set(dep)
        op["tiles"] = set(a["n"] for a, w in acc if a["n"][:3] == "ps:")
    users = {}
    for op in ops:
        for t in op["tiles"]:
            users.setdefault(t, []).append(op["id"])
    succ = [[] for o in ops]
    for op in ops:
        for d in op["dep"]:
            succ[d].append(op["id"])
    X, SAME = opt["X"], opt["same"]
    for op in reversed(ops):
        op["pr"] = op["c"] + op.get("lat", 0) + max([ops[s]["pr"] + X for s in succ[op["id"]]] + [0])
    free = dict((e, 0.0) for e in "VSPQY")
    left = [len(o["dep"]) for o in ops]
    ready = [o["id"] for o in ops if not o["dep"]]
    bank_of, tenant, order = {}, [None] * 8, []
    done = set()

    def gap(a, b):
        if a.get("id") in b.get("lag", ()):
            return 0
        return a.get("lat", 0) + (0 if a["e"] == b["e"] == "P" else SAME if a["e"] == b["e"] and "lat" not in a else X)

    def avail(op, extra=()):
        t = 0.0
        for d in list(op["dep"]) + list(extra):
            t = max(t, ops[d]["st"] + ops[d]["c"] + gap(ops[d], op))
        return t
    pr = [op["pr"] + opt["bias"] * (op["ch"] == 0) for op in ops]
    while ready:
        cand = []
        for i in ready:
            op = ops[i]
            new = [t for t in op["tiles"] if t not in bank_of]
            extra, pick = [], None
            if new:
                cands = [b for b in range(8) if tenant[b] is None or all(x in done for x in users[tenant[b]])]
                if not cands:
                    continue
                pick = min(cands, key=lambda b: 0 if tenant[b] is None else max(ops[x]["end"] for x in users[tenant[b]]))
                extra = [x for x in users[tenant[pick]]] if tenant[pick] else []
            st = max(free[op["e"]], avail(op, extra))
            cand.append((st, i, op, new, pick, extra))
        first = min(cand, key=lambda x: x[:2])
        lim = first[0] + opt["th"] * first[2]["c"] + 30
        st, i, op, new, pick, extra = max([x for x in cand if x[2]["e"] == first[2]["e"] and x[0] <= lim],
                                          key=lambda x: (pr[x[1]], -x[1]))
        if new:
            bank_of[new[0]] = pick
            tenant[pick] = new[0]
            op["dep"] = op["dep"] | set(extra)
        op["st"] = st
        free[op["e"]] = st + op["c"]
        op["end"] = st + op["c"] + op.get("lat", 0)
        order.append(op)
        done.add(op["id"])
        ready.remove(op["id"])
        for s in succ[op["id"]]:
            left[s] -= 1
            if left[s] == 0:
                ready.append(s)
    net = network(ops, gap)
    perm = improve(net, [op["id"] for op in order], opt)
    res = replay(net, perm, [fresh(net)], 0)
    order, bank_of, tenant = [ops[i] for i in perm], {}, [None] * 8
    for op in order:
        op["dep"] = set(op["dep0"]) - set(op.get("lag", ()))
        op["st"] = res[3][op["id"]] - op["c"]
        op["end"] = res[3][op["id"]] + op.get("lat", 0)
        for t in op["tiles"]:
            if t not in bank_of:
                b = bank_of[t] = res[4][net["tile"][op["id"]]]
                op["dep"] |= set(users.get(tenant[b], ()))
                tenant[b] = t
    cnt = dict((e, 0) for e in "VSPQ")
    for op in order:
        if "sem" not in op:
            cnt[op["e"]] += 1
            op["sig"] = (op["e"], cnt[op["e"]])
        else:
            op["sig"] = (op["sem"], 16 if op["ins"][0][0] == "dma" else 2 * opt["eng"])
    seen = dict((e, {}) for e in "VSPQY")
    for op in order:
        need = {}
        for d in op["dep"]:
            s, v = ops[d]["sig"]
            if not ops[d]["e"] == "P" == op["e"] and need.get(s, (0, 0))[0] < v:
                need[s] = (v, d)
        mine = seen[op["e"]]
        op["waits"] = []
        for s, (v, d) in sorted(need.items(), key=lambda x: -ops[x[1][1]]["end"]):
            if mine.get(s, 0) < v:
                op["waits"].append((s, v))
                mine[s] = v
                for s2, v2 in ops[d]["known"].items() if opt["clock"] else ():
                    mine[s2] = max(mine.get(s2, 0), v2)
        op["known"] = dict(mine)
    return order, bank_of, cnt


PLAN = {}


def plan():
    if not PLAN:
        ops = build(OPT)
        PLAN["p"] = schedule(ops, OPT)
    return PLAN["p"]


def helper_of(src, dst, T, topo):
    if topo.may_write(src, dst):
        return dst
    c = [x for x in topo.cores_of(src) if T.rank_of(x) is None and topo.may_write(x, dst)]
    c.sort(key=lambda x: topo.die(x) != topo.die(src))
    return c[0]


def bits(engines):
    m = 0
    for e in engines:
        m |= 1 << e
    return m


def rank_program(g, core, T, topo):
    order, bank_of, cnt = plan()
    n, ne = len(T.cores), OPT["eng"]
    msgs = [op["ins"][0][1][2] for op in order if op["ins"][0][0] == "xfer"]
    rank = T.rank_of(core)
    if rank is None:
        for r in range(n):
            for side, (lo, hi) in ((-1, (1152, 1280)), (1, (0, 128))):
                src, dst = T.cores[r], T.cores[(r + side) % n]
                if helper_of(src, dst, T, topo) != core:
                    continue
                rid, pid = topo.addr(dst, core)
                eng = topo.engines(core, dst)[:ne]
                for u in msgs:
                    g.wait_ge(T.sem["h" + u], ne)
                    buf = T["R" + u][:, lo:hi]
                    g.remote_dma(buf, buf, T.sem["h" + u], T.sem.sent, pid, rid, bits(eng))
                g.wait_ge(T.sem.sent, ne * len(msgs))
        return
    Q = {"V": g.vector, "S": g.scalar, "P": g.tensor, "Q": g, "Y": g.sync}

    def real(a):
        if not isinstance(a, dict):
            return a
        if "win" in a:
            return real(a["win"]).indirect(real(a["off"]))
        nm = a["n"]
        if nm[:3] == "ps:":
            nm = "bank%d" % bank_of[nm]
        return T[nm][a["i"]]
    for op in order:
        q = Q[op["e"]]
        for s, v in op["waits"]:
            q.wait_ge(T.sem[s], v)
        last = None
        for kind, args in op["ins"]:
            if kind == "xfer":
                u = args[2]
                tr, used = [], []
                for side, (lo, hi), s0 in ((-1, (1152, 1280), 0), (1, (0, 128), 64)):
                    to = helper_of(core, T.cores[(rank + side) % n], T, topo)
                    eng = [e for e in topo.engines(core, to) if e not in used][:ne]
                    used.extend(eng)
                    rid, pid = topo.addr(to, core)
                    tr.append(RemoteDMATransfer(dst_ids=[DstId(rid=rid, pnc=pid)], dma_engine_mask=bits(eng),
                                                remote_sem=T.sem["h" + u], src=T["S" + u][:, s0:s0 + 128],
                                                dst=T["R" + u][:, lo:hi]))
                g.remote_dma_fused(tr, local_sem=T.sem.sent)
                continue
            if kind == "none":
                continue
            if kind == "dma":
                o, i = args[2]
                o = real(o) if isinstance(o, dict) else T[o[0]][:, o[1]:o[2]]
                i = real(i) if isinstance(i, dict) else T[i[0]][:] if len(i) == 1 else T[i[0]][:, i[1]:i[2]]
                q.dma_start(o, i).then_inc(T.sem[op["sem"]], 16)
                continue
            a = [real(x) for x in args]
            if kind == "tt":
                last = q.tensor_tensor(a[0], a[1], a[2], a[3])
            elif kind == "ts":
                last = q.tensor_scalar(*(a if a[5] is not None else a[:5]))
            elif kind == "cp":
                last = q.tensor_copy(a[0], a[1])
            elif kind == "ms":
                last = q.memset(a[0], a[1])
            elif kind == "rcp":
                last = q.reciprocal(a[0], a[1])
            elif kind == "scan":
                last = q.tensor_tensor_scan(a[0], a[1], a[2], 0.0, A.max, A.min)
            elif kind == "act":
                last = q.activation(a[0], a[1], a[2], bias=a[3], scale=a[4])
            elif kind == "mm":
                last = q.matmul(a[0], a[1], a[2], a[3], a[4])
            elif kind == "sel":
                last = q.affine_select(*a)
            elif kind == "iota":
                if SCRATCH[args[0]["n"]][2] == I32:
                    last = q.iota(*a)
                else:
                    last = q.iota(a[0], a[1], a[2], a[3], allow_small_or_imprecise_dtypes=True)
        if last is not None:
            last.then_inc(T.sem[op["e"]], 1)
    for e in "VSPQ":
        g.wait_ge(T.sem[e], cnt[e])
    for s in DMAS:
        g.wait_ge(T.sem[s], 16)
    for u in msgs:
        g.wait_ge(T.sem["h" + u], 2 * ne)
    g.wait_ge(T.sem.sent, 2 * ne * len(msgs))
